import numpy as np, ml_dtypes
CORES = [1,5,17,21,33,37,49,53]
N = 8
import mx_ref
BF = ml_dtypes.bfloat16
def gentries(a):
    return np.ascontiguousarray(a.reshape(8, 16, -1).transpose(0, 2, 1)).reshape(8, -1)
def gtable(e):
    e = np.asarray(e); return np.ascontiguousarray(e.reshape(8, -1, 16).transpose(0, 2, 1)).reshape(128, -1).astype(np.int32)
def gcols(t, e):
    v = np.concatenate([t.reshape(8, 16, -1, 4), np.zeros((8, 16, 1, 4), BF)], axis=2)
    return np.ascontiguousarray(np.stack([v[g][:, e[g]] for g in range(8)])).reshape(128, -1)
def tile(rs):
    return np.stack(rs, axis=2).reshape(128, -1).astype(BF)
def pick(q, e):
    c = np.concatenate([q[0].reshape(128, -1, 4), np.zeros((128, 1, 4), np.uint8)], axis=1); s = np.concatenate([q[1], np.ones((16, 1), np.uint8)], axis=1)
    return (np.ascontiguousarray(c[:, e].reshape(128, -1)), np.ascontiguousarray(s[:, e]))
def join(*qs):
    return (np.concatenate([q[0] for q in qs], axis=1), np.concatenate([q[1] for q in qs], axis=1))
def put(q, e, v):
    c, s = q[0].reshape(128, -1, 4).copy(), q[1].copy(); c[:, e] = v[0].reshape(128, -1, 4); s[:, e] = v[1]
    return (c.reshape(128, -1), s)
def pk(c, s):
    return (np.ascontiguousarray(c), mx_ref.live(s))
def emit(q):
    return q[0], q[1]
def packed(v, rng):
    q = [mx_ref.quantize(np.ascontiguousarray(v[r])) for r in range(N)]
    return np.stack([a for a, b in q]), np.stack([mx_ref.plane(b, rng) for a, b in q])
def values_of_codes():
    e, c = np.zeros((128, 128, 4), np.float32), np.zeros((128, 2, 4), np.uint8)
    e[np.arange(128), np.arange(128), 0] = 1
    c[:127, :, 0] = np.arange(256).reshape(2, 128).T[:127]
    return mx_ref.matmul(mx_ref.quantize(e.reshape(128, 512).astype(BF)), (c.reshape(128, 8), np.full((16, 2), 127, np.uint8))).T.reshape(-1).astype(np.float64)
CODE_VALUE, SCALE_VALUE = values_of_codes(), 2.0 ** (np.arange(256) - 127.0)
def decode(q):
    return (CODE_VALUE[q[0]].reshape(16, 8, -1, 4) * SCALE_VALUE[q[1]][:, None, :, None] + 0.0).reshape(128, -1).astype(np.float32)
def f(rng, *shape):
    return mx_ref.flush((rng.standard_normal(shape, dtype=np.float32) * np.exp2(rng.integers(-2, 3, shape[:-1] + (1,)))).astype(BF))
def wide(rng, *shape, cols=0):
    v = rng.standard_normal(shape, dtype=np.float32) * np.exp2(rng.integers(-12, 13, shape)).astype(np.float32)
    if cols: v *= np.repeat(np.exp2(rng.integers(-cols, cols + 1, shape[:-2] + (1, shape[-1] // 4))) * (rng.random(shape[:-2] + (1, shape[-1] // 4)) > 0.0625), 4, axis=-1).astype(np.float32)
    return mx_ref.flush(v.astype(BF))
C, S, R = 256, 64, 3
L = 3 * C + 2 * S
def flipped(t, pos):
    h, a = np.arange(3 * C), t[:, :3 * C]
    o = np.where(a < 3 * C, a, h) // 3
    low = np.minimum(a, h)
    wants = np.take_along_axis(pos, o, axis=1) != np.repeat(pos, 3, axis=1)
    least = np.min(np.where(wants, low, L).reshape(8, C, 3), axis=2)
    go = wants & (h < a) & (low == np.repeat(least, 3, axis=1)) & (low == np.take_along_axis(least, o, axis=1))
    g, i = np.nonzero(go)
    j = a[g, i]
    i1, i2 = i // 3 * 3 + (i + 1) % 3, i // 3 * 3 + (i + 2) % 3
    j1, j2 = j // 3 * 3 + (j + 1) % 3, j // 3 * 3 + (j + 2) % 3
    phi = np.tile(np.arange(L), (8, 1))
    phi[g, i2] = i1
    phi[g, j1] = i2
    phi[g, j2] = j1
    phi[g, i1] = j2
    new = np.zeros_like(t)
    np.put_along_axis(new, phi, np.take_along_axis(phi, t, axis=1), axis=1)
    return new
def anyhow(rng):
    return np.argsort(rng.random((N, 8, 3 * C)), axis=2)
def strip(rng, q):
    return np.concatenate([rng.permutation(3 * q + 2), np.stack([3 * q + 1, 3 * np.roll(q, -1)], axis=1).reshape(-1)])
def pairs(rng):
    q = rng.permutation(C).reshape(2, C // 2)
    k = np.argsort(rng.random((C // 2, 3)), axis=1)
    e = np.stack([3 * q[0][:, None] + np.arange(3), 3 * q[1][:, None] + k], axis=2)
    kept = np.ones((C // 2, 3), bool)
    kept[rng.permutation(C // 2)[:S], rng.integers(0, 3, S)] = False
    return np.concatenate([rng.permutation(e[~kept].reshape(-1)), e[kept].reshape(-1)]), q[0], q[1]
def joined(p):
    s = np.broadcast_to(3 * C + np.arange(2 * S), (N, 8, 2 * S))
    a = np.concatenate([p[:, :, :2 * S], p[:, :, 2 * S::2]], axis=2)
    b = np.concatenate([s, p[:, :, 2 * S + 1::2]], axis=2)
    e = np.zeros((N, 8, L), np.int64)
    np.put_along_axis(e, a, b, axis=2)
    np.put_along_axis(e, b, a, axis=2)
    return np.stack([gtable(k) for k in e])
def drawn(rng, x, p, u, v, w):
    c, s = packed(w, rng)
    return {"x": x, "tw": joined(p), "u": u, "v": v, "wc": c, "ws": s}
def setup_inputs(rng):
    return drawn(rng, np.array(f(rng, N, 128, 4 * C)), anyhow(rng), np.array(f(rng, N, 128, 512)), np.array(f(rng, N, 128, 512)), np.array(f(rng, N, 128, 2048)))
def setup_inputs_near(rng):
    p = anyhow(rng)
    o = rng.permutation(N)
    c = rng.integers(-1, 2, (N, 8, R, C)).astype(np.float32)
    for r in range(N):
        if o[r] == 0:
            for g in range(8): p[r, g] = strip(rng, np.arange(C))
            c[r, :, 0] = -np.abs(c[r, :, 0])
            c[r, :, 0, ::2] = 1
        if o[r] == 1: c[r] = -np.abs(c[r])
        if o[r] == 2: c[r] = 1
        if o[r] == 3:
            for g in rng.permutation(8)[:4]:
                p[r, g], a, b = pairs(rng)
                c[r, g, 0] = -np.abs(c[r, g, 0])
                c[r, g, 0, a] = 1
    x = np.array(f(rng, N, 128, 4 * C)).astype(np.float32).reshape(N, 8, 16, C, 4)
    x[:, :, :8] = 0
    x[:, :, :R, :, 0] = c * np.exp2(np.array([-30.0, -12.0, 0.0, 10.0]))[rng.integers(0, 4, (N, 8, 1, C))]
    k = np.where(rng.permutation(N) < N // 2, 2.0 ** -30, 1.0).astype(np.float32).astype(BF)
    u = np.array(f(rng, N, 128, 512)).reshape(N, 128, 128, 4)
    for g in range(8):
        for i in range(16 * g, 16 * g + R):
            u[:, :, i] = 0
            u[:, i, i, 0] = k
    w = np.array(f(rng, N, 128, 2048)).reshape(N, 8, 16, 4, 8, 16, 4)
    w[:, :, :8] = 0
    w[:, :, :, :, :, :8] = 0
    return drawn(rng, x.reshape(N, 128, 4 * C).astype(BF), p, u.reshape(N, 128, 512), np.array(f(rng, N, 128, 512)), w.reshape(N, 128, 2048))
def setup_inputs_loops(rng):
    p = anyhow(rng)
    o = rng.permutation(N)
    n = (2 * S + 5) // 6 * 2
    three = np.arange(3)
    x = np.array(f(rng, N, 128, 4 * C)).reshape(N, 128, C, 4)
    for r in range(N):
        if o[r] % 3 == 2: x[r, :, ::C - 1] = BF(-2.0 ** 26)
        for g in range(8):
            q = rng.permutation(C)
            if o[r] % 3 == 0: p[r, g] = (3 * q[:, None] + three).reshape(-1)
            if o[r] % 3 == 1:
                a, b = q[n::2], q[n + 1::2]
                k = np.argsort(rng.random((len(a), 3)), axis=1)
                e = np.stack([3 * a[:, None] + three, 3 * b[:, None] + k], axis=2)
                p[r, g] = np.concatenate([(3 * q[:n, None] + three).reshape(-1), e.reshape(-1)])
            if o[r] % 3 == 2: p[r, g] = strip(rng, q)
    return drawn(rng, x.reshape(N, 128, 4 * C), p, np.array(f(rng, N, 128, 512)), np.array(f(rng, N, 128, 512)), np.array(f(rng, N, 128, 2048)))
def setup_inputs_huge(rng):
    o = rng.permutation(N)
    x = -2.0 ** 30 * np.where(rng.random((N, 128, 4 * C)) < 0.75, 1.0, 0.5 + 0.4 * rng.random((N, 128, 4 * C)))
    x[:, 15::16] = 2.0 ** 30 * np.where(rng.random((N, 8, 4 * C)) < 0.75, -1.0, 0.5)
    s = np.argsort(rng.random((N, 128, 128)), axis=1) % 2 * 2.0 - 1.0
    s[o == 0] = 1
    s[o == 1] = -1
    u = 2.0 ** 30 * (0.75 + 0.25 * rng.random((N, 128, 128, 4))) * s[:, :, :, None]
    w = np.zeros((N, 128, 4, 128, 4), np.float32)
    i = np.arange(128)
    for b in range(4): w[:, i, b, i, b] = np.where(i % 16 == 15, -8, -24)
    return drawn(rng, x.astype(np.float32).astype(BF), anyhow(rng), u.astype(np.float32).reshape(N, 128, 512).astype(BF), np.array(f(rng, N, 128, 512)), w.reshape(N, 128, 2048).astype(BF))
def setup_inputs_spread(rng):
    d = setup_inputs(rng)
    d["x"] = np.array(wide(rng, N, 128, 4 * C, cols=6))
    return d
def check_inputs(d):
    b = []
    for k in ("x", "u", "v"):
        a = np.abs(d[k].astype(np.float32))
        if not (np.isfinite(a).all() and ((a == 0) | (a >= 2.0 ** -30) & (a <= 2.0 ** 30)).all()): b.append("a value of " + k)
    for r in range(N):
        t = gentries(d["tw"][r]).astype(np.int64)
        if ((t < 0) | (t >= L)).any(): b.append("an entry of tw")
        t = np.clip(t, 0, L - 1)
        if (np.take_along_axis(t, t, axis=1) != np.arange(L)).any(): b.append("tw: a twin's twin")
        if (t == np.arange(L)).any(): b.append("tw: a number is its own twin")
        if (t[:, 3 * C:] >= 3 * C).any(): b.append("tw: a slot's twin is a slot")
    return b
def reference(x, tw, u, v, wc, ws):
    qu = [mx_ref.quantize(u[r]) for r in range(N)]
    lay = [pk(wc[r], ws[r]) for r in range(N)]
    now = [x[r] for r in range(N)]
    twin = [gentries(tw[r]).astype(np.int64) for r in range(N)]
    for t in range(R):
        held, right, left = [], [], []
        for r in range(N):
            q = mx_ref.quantize(now[r])
            twin[r] = flipped(twin[r], mx_ref.matmul(qu[r], q)[t::16] > 0)
            held.append(decode(q))
            e = twin[r][:, 3 * C:] // 3
            right.append(mx_ref.quantize(gcols(now[r], e[:, :S])))
            left.append(mx_ref.quantize(gcols(now[r], e[:, S:])))
        for r in range(N):
            came = decode(join(left[(r + 1) % N], right[(r - 1) % N]))
            z = np.concatenate([held[r], came], axis=1).astype(BF)
            a = twin[r][:, :3 * C]
            e = np.where(a < 3 * C, a // 3, a - 2 * C)
            p = [gcols(z, e[:, k::3]).astype(np.float32) for k in range(3)]
            q = mx_ref.quantize(np.maximum(np.maximum(p[0], p[1]), p[2]).astype(BF))
            now[r] = tile([held[r][:, b::4] + np.maximum(mx_ref.matmul(pick(lay[r], np.arange(128 * b, 128 * b + 128)), q), np.float32(0.0)) * np.float32(0.015625) for b in range(4)])
    y, ot = np.zeros((N, 128, C), np.float32), np.zeros((N, 8, L), np.float32)
    oc, osc = np.zeros((N, 128, 4 * C), np.uint8), np.zeros((N, 16, C), np.uint8)
    for r in range(N):
        q = mx_ref.quantize(now[r])
        y[r] = mx_ref.matmul(mx_ref.quantize(v[r]), q)
        ot[r] = twin[r]
        oc[r], osc[r] = emit(q)
    return {"y": y, "ot": ot, "oc": oc, "osc": osc}

@@ -1,0 +1,538 @@
+from concourse.bass import DstId, RemoteDMATransfer
+from concourse.mybir import dt, AluOpType, ActivationFunctionType
+
+ROUNDS = 3
+ZW = 896
+
+SCRATCH = {
+    "xin": ("sbuf", [128, 1024], "bfloat16"),
+    "uin": ("sbuf", [128, 512], "bfloat16"),
+    "vin": ("sbuf", [128, 512], "bfloat16"),
+    "xt": ("sbuf", [128, 3072], "bfloat16"),
+    "mt": ("sbuf", [128, 3072], "bfloat16"),
+    "z": ("sbuf", [128, 12 * ZW], "bfloat16"),
+    "nz": ("sbuf", [128, 12 * 512], "bfloat16"),
+    "ma": ("sbuf", [128, 1536], "bfloat16"),
+    "mb": ("sbuf", [128, 1536], "bfloat16"),
+    "mg": ("sbuf", [128, 4608], "bfloat16"),
+    "ms": ("sbuf", [128, 4608], "bfloat16"),
+    "m3": ("sbuf", [128, 768], "bfloat16"),
+    "tm": ("sbuf", [128, 1024], "float32"),
+    "yo": ("sbuf", [128, 256], "float32"),
+    "ones": ("sbuf", [128, 512], "bfloat16"),
+    "ec": ("sbuf", [128, 2048], "bfloat16"),
+    "qe": ("sbuf", [128, 512], "float8_e4m3fn_x4"), "se": ("sbuf", [128, 512], "uint8"),
+    "qu": ("sbuf", [128, 128], "float8_e4m3fn_x4"), "su": ("sbuf", [128, 128], "uint8"),
+    "qp": ("sbuf", [128, 384], "float8_e4m3fn_x4"), "sp": ("sbuf", [128, 384], "uint8"),
+    "qv": ("sbuf", [128, 128], "float8_e4m3fn_x4"), "svp": ("sbuf", [128, 128], "uint8"),
+    "qw": ("sbuf", [128, 512], "float8_e4m3fn_x4"), "sw": ("sbuf", [128, 512], "uint8"),
+    "qx": ("sbuf", [128, 1024], "float8_e4m3fn_x4"), "sx": ("sbuf", [128, 1024], "uint8"),
+    "qm": ("sbuf", [128, 768], "float8_e4m3fn_x4"), "sm": ("sbuf", [128, 768], "uint8"),
+    "lq": ("sbuf", [128, 1536], "float8_e4m3fn_x4"), "lsc": ("sbuf", [128, 1536], "uint8"),
+    "twi": ("sbuf", [128, 56], "int32"),
+    "fl": ("sbuf", [128, 24000], "float32"),
+    "il": ("sbuf", [128, 1800], "int32"),
+    "bl": ("sbuf", [128, 8800], "bfloat16"),
+    "ul": ("sbuf", [128, 1800], "uint16"),
+    "snd": ("sbuf", [128, 48], "uint16"),
+    "lnd": ("sbuf", [128, 24], "uint16"),
+    "ps": ("psum", [128, 4096], "float32"),
+}
+SEMAPHORES = (["sv", "ss", "st", "sg", "loc", "out"] + ["ld%d" % i for i in range(6)] + ["zd%d" % i for i in range(12)]
+              + ["aq%d" % t for t in range(3)] + ["al%d" % t for t in range(3)])
+
+
+def rank_program(g, core, T, topo):
+    rank = T.rank_of(core)
+    if rank is None:
+        return
+    A = AluOpType
+    AF = ActivationFunctionType
+    cores = T.cores
+    n = len(cores)
+    up, down = cores[(rank + 1) % n], cores[(rank + n - 1) % n]
+
+    queues = {"v": g.vector, "s": g.scalar, "t": g.tensor, "g": g, "y": g.sync}
+    qsem = {"v": "sv", "s": "ss", "t": "st", "g": "sg"}
+    total = {}
+    known = {q: {} for q in queues}
+    touched = {}
+
+    def span(r):
+        if r[0] == "ps":
+            return r[1] // 512 * 512, (r[2] + 511) // 512 * 512
+        return r[1], r[2]
+
+    def needs(q, dma, ins, outs):
+        found = []
+        for writing, regs in ((False, ins), (True, outs)):
+            for r in regs:
+                a, b = span(r)
+                for (c, d, w, oq, odma, op) in touched.get(r[0], ()):
+                    if c >= b or d <= a:
+                        continue
+                    same = oq == q and not odma and not dma
+                    if r[0] == "ps":
+                        if same and (writing or not w):
+                            continue
+                    else:
+                        if not writing and not w:
+                            continue
+                        if same and writing:
+                            continue
+                    found.append(op)
+        return found
+
+    def wait_for(q, ops):
+        want = {}
+        for op in ops:
+            s = op["sem"]
+            if known[q].get(s, 0) >= op["cnt"]:
+                continue
+            cnt = op["cnt"] if s in ("sv", "ss", "st", "sg") else max(op["cnt"], total.get(s, 0))
+            if s not in want or want[s][0] < cnt:
+                want[s] = (cnt, op["clk"])
+        for s in list(want):
+            if any(s2 != s and want[s2][1].get(s, 0) >= want[s][0] for s2 in want):
+                del want[s]
+        for s in sorted(want):
+            queues[q].wait_ge(T.sem[s], want[s][0])
+        for op in ops:
+            for k, c in op["clk"].items():
+                if known[q].get(k, 0) < c:
+                    known[q][k] = c
+        for s in want:
+            if known[q].get(s, 0) < want[s][0]:
+                known[q][s] = want[s][0]
+
+    def note(q, dma, ins, outs, op):
+        for w, regs in ((False, ins), (True, outs)):
+            for r in regs:
+                a, b = span(r)
+                touched.setdefault(r[0], []).append((a, b, w, q, dma, op))
+
+    def run(q, fn, outs, ins):
+        wait_for(q, needs(q, False, ins, outs))
+        s = qsem[q]
+        total[s] = total.get(s, 0) + 1
+        fn().then_inc(T.sem[s], 1)
+        clk = dict(known[q])
+        clk[s] = total[s]
+        note(q, False, ins, outs, {"sem": s, "cnt": total[s], "clk": clk})
+
+    def dma(q, out_ap, in_ap, outs, ins, sem):
+        wait_for(q, needs(q, True, ins, outs))
+        total[sem] = total.get(sem, 0) + 16
+        queues[q].dma_start(out_ap, in_ap).then_inc(T.sem[sem], 16)
+        note(q, True, ins, outs, {"sem": sem, "cnt": total[sem], "clk": dict(known[q])})
+
+    def arrive(sem, cnt, outs):
+        total[sem] = total.get(sem, 0) + cnt
+        note("net", True, [], outs, {"sem": sem, "cnt": total[sem], "clk": {}})
+
+    def ap(r):
+        if len(r) > 3 and r[3] != 1:
+            return T[r[0]][:, r[1]:r[2]:r[3]]
+        return T[r[0]][:, r[1]:r[2]]
+
+    def u8(r):
+        return ap(r).bitcast(dt.uint8)
+
+    unit = {"fl": 16, "il": 16, "bl": 32, "ul": 32, "snd": 16}
+    free = {b: 0 for b in unit}
+
+    def new(buf, w):
+        a = free[buf]
+        free[buf] = a + (w + unit[buf] - 1) // unit[buf] * unit[buf]
+        if free[buf] > SCRATCH[buf][1][1]:
+            raise ValueError(buf)
+        return (buf, a, a + w)
+
+    def sub(r, a, b, s=1):
+        return (r[0], r[1] + a, r[1] + b, s)
+
+    def blk(r, k, w=256):
+        return sub(r, w * k, w * k + w)
+
+    def reg(name, k, w):
+        return (name, w * k, w * k + w)
+
+    def num(x, ins):
+        if isinstance(x, tuple):
+            ins.append(x)
+            return ap(x)
+        return x
+
+    def ts(out, in0, s1, op0, s2=None, op1=None):
+        ins = [in0]
+        a1 = num(s1, ins)
+        a2 = num(s2, ins)
+        if op1 is None:
+            run("v", lambda: g.vector.tensor_scalar(ap(out), ap(in0), a1, None, op0), [out], ins)
+        else:
+            run("v", lambda: g.vector.tensor_scalar(ap(out), ap(in0), a1, a2, op0, op1), [out], ins)
+
+    def tt(out, in0, in1, op):
+        run("v", lambda: g.vector.tensor_tensor(ap(out), ap(in0), ap(in1), op), [out], [in0, in1])
+
+    def vcopy(out, in0):
+        run("v", lambda: g.vector.tensor_copy(ap(out), ap(in0)), [out], [in0])
+
+    def fill(out, x):
+        run("v", lambda: g.vector.memset(ap(out), x), [out], [])
+
+    def scan(out, d0, d1, op0=A.mult, op1=A.max):
+        run("v", lambda: g.vector.tensor_tensor_scan(ap(out), ap(d0), ap(d1), 0.0, op0, op1), [out], [d0, d1])
+
+    def scopy(out, in0, bias=None, scale=1.0):
+        if bias is None:
+            run("s", lambda: g.scalar.activation(ap(out), ap(in0), AF.Copy), [out], [in0])
+        else:
+            run("s", lambda: g.scalar.activation(ap(out), ap(in0), AF.Identity, bias=bias, scale=scale), [out], [in0])
+
+    def vget(out, win, off):
+        run("v", lambda: g.vector.tensor_copy(ap(out), ap(win).indirect(ap(off))), [out], [win, off])
+
+    def sget(out, win, off):
+        run("s", lambda: g.scalar.activation(ap(out), ap(win).indirect(ap(off)), AF.Copy), [out], [win, off])
+
+    def vmax(out, win, off, in1):
+        run("v", lambda: g.vector.tensor_tensor(ap(out), ap(win).indirect(ap(off)), ap(in1), A.max), [out], [win, off, in1])
+
+    def iota(out, pattern, base, cm, flag=False):
+        if flag:
+            run("g", lambda: g.iota(ap(out), pattern, base, cm, allow_small_or_imprecise_dtypes=True), [out], [])
+        else:
+            run("g", lambda: g.iota(ap(out), pattern, base, cm), [out], [])
+
+    def quant(codes, scales, tile):
+        run("v", lambda: g.vector.quantize_mx(ap(codes), ap(scales), ap(tile)), [codes, scales], [tile])
+
+    def mm(bank, w, ws, x, xs, width):
+        out = ("ps", 512 * bank, 512 * bank + width)
+        run("t", lambda: g.tensor.matmul_mx(ap(out), ap(w), ap(ws), ap(x), ap(xs), True, True), [out], [w, ws, x, xs])
+
+    full = lambda name, w: (name, 0, w)
+    dma("y", T.twi[:, :], T.tw[:, :], [full("twi", 56)], [], "ld0")
+    dma("s", T.xin[:, :], T.x[:, :], [full("xin", 1024)], [], "ld1")
+    dma("y", T.uin[:, :], T.u[:, :], [full("uin", 512)], [], "ld2")
+    dma("y", T.qw[:, :].bitcast(dt.uint8), T.wc[:, :], [full("qw", 512)], [], "ld3")
+    dma("y", T.sw[:, :], T.ws[:, :], [full("sw", 512)], [], "ld4")
+    dma("y", T.vin[:, :], T.v[:, :], [full("vin", 512)], [], "ld5")
+
+    pcol = new("il", 1)
+    jrow = new("bl", 128)
+    base = new("fl", 256)
+    uo_i, id_i, nat_i = new("il", 24), new("il", 48), new("il", 48)
+    iota(pcol, [[0, 1]], 0, 1)
+    iota(jrow, [[0, 8], [1, 16]], 0, 0, True)
+    iota(base, [[1, 256]], 1024, 0, True)
+    iota(uo_i, [[1, 3], [16, 8]], 0, 0)
+    iota(id_i, [[256, 3], [16, 16]], 0, 0)
+    iota(nat_i, [[1, 3], [48, 16]], 0, 0)
+    fill(full("ones", 512), 1.0)
+    for b in range(4):
+        e = reg("ec", b, 512)
+        run("g", lambda: g.affine_select(ap(e), T.ones[:, :], [[1, 512]], A.is_equal, 0.0, -b, -4), [e], [full("ones", 512)])
+
+    icol_i, icol = new("il", 1), new("fl", 1)
+    ts(icol_i, pcol, 15, A.bitwise_and)
+    vcopy(icol, icol_i)
+    mask = new("bl", 256)
+    ts(sub(mask, 0, 128), jrow, icol, A.is_gt, 2.0, A.mult)
+    half, hit, one = new("fl", 16), new("fl", 16), new("fl", 16)
+    fill(half, 0.5)
+    fill(one, 1.0)
+    ts(hit, sub(jrow, 0, 16), icol, A.is_equal)
+    vcopy(sub(mask, 128, 256), sub(mask, 0, 128))
+    dsc_r, thr_r = new("fl", 16), new("fl", 16)
+    scan(dsc_r, half, hit, A.mult, A.add)
+    scan(thr_r, sub(mask, 0, 16), one)
+    dsc, thr = sub(dsc_r, 15, 16), sub(thr_r, 15, 16)
+
+    natinv = new("fl", 896)
+    for k in range(3):
+        ts(sub(natinv, k, 768, 3), base, 256.0 * k, A.add)
+    ts(sub(natinv, 768, 896), sub(base, 0, 128), 768.0, A.add)
+    ftab, nattab = new("fl", 1792), new("fl", 896)
+    fr = [new("fl", 896) for t in range(ROUNDS)]
+
+    def table(a, b):
+        for i in range(a, b):
+            scopy(blk(ftab, i), base, float([0, 256, 512, 768, 512, 0, 256][i]))
+    table(0, 3)
+
+    trn = new("fl", 896)
+    tw_o = new("ul", 56)
+    vcopy(tw_o, full("twi", 56))
+    sget(trn, natinv, tw_o)
+    uo, idg, ic3 = new("ul", 24), new("il", 48), new("fl", 1)
+    own_a, own, c1, c2, c3, c4 = [new("fl", 48) for i in range(6)]
+    vcopy(uo, uo_i)
+    ts(idg, id_i, icol, A.add)
+    ts(ic3, icol, 3.0, A.mult)
+    ts(own_a, nat_i, -1.0, A.mult, 1023.0, A.add)
+    fill(sub(c2, 0, 16), 512.0)
+    fill(sub(c2, 16, 48), -256.0)
+    ts(own, own_a, ic3, A.subtract)
+    ts(c1, idg, -1.0, A.mult, 1024.0, A.add)
+    fill(sub(c3, 0, 32), 256.0)
+    fill(sub(c3, 32, 48), -512.0)
+    ts(c4, idg, -1.0, A.mult, 256.0, A.add)
+
+    tix = [new("il", 80) for t in range(ROUNDS)]
+    toff = [new("ul", 64) for t in range(ROUNDS + 1)]
+    fa, fb = [new("fl", 48) for t in range(ROUNDS)], [new("fl", 48) for t in range(ROUNDS)]
+    keys = [new("fl", 48) for t in range(ROUNDS)]
+    ooff = [new("ul", 48) for t in range(ROUNDS)]
+    oth = [new("il", 48) for t in range(ROUNDS)]
+
+    def decode(out, sc, a, b):
+        ts(out, sub(sc, a + 15, b, 16), dsc, A.mult, 1024.0, A.subtract)
+
+    def lists_first(t, sc):
+        own_t = sub(tix[t], 0, 48)
+        decode(own_t, sc, 0, 768)
+        ts(oth[t], own_t, 255, A.bitwise_and)
+        vcopy(ooff[t], oth[t])
+
+    def lists_rest(t, sc):
+        ti, o = tix[t], oth[t]
+        own_t = sub(ti, 0, 48)
+        hi = new("il", 48)
+        n1, n2, lt, n3, n4, o1 = [new("fl", 48) for i in range(6)]
+        ts(hi, own_t, 8, A.logical_shift_right)
+        ts(n1, o, -3.0, A.mult, 1023.0, A.add)
+        ts(lt, own_t, 768.0, A.is_lt, 512.0, A.mult)
+        ts(o1, o, 0.001953125, A.mult)
+        tt(n2, n1, hi, A.subtract)
+        decode(sub(ti, 48, 80), sc, 0, 512)
+        tt(n3, n2, own, A.max)
+        tt(fb[t], sub(ti, 16, 64), c4, A.add)
+        tt(n4, n3, o1, A.add)
+        tt(fa[t], sub(ti, 32, 80), c1, A.add)
+        tt(keys[t], n4, lt, A.mult)
+
+    def pick_u(t):
+        off = blk(uo, t, 8)
+        c, d = 128 * t, 128 * t + 128
+        run("v", lambda: g.vector.tensor_copy(T.qp[:, c:d].bitcast(dt.uint32), T.qu[:, 0:128].bitcast(dt.uint32).indirect(ap(off))),
+            [("qp", c, d)], [("qu", 0, 128), uo])
+        run("s", lambda: g.scalar.activation(T.sp[:, c:d], T.su[:, 0:128].indirect(ap(off)), AF.Copy), [("sp", c, d)], [("su", 0, 128), uo])
+
+    quant(full("qu", 128), full("su", 128), full("uin", 512))
+    quant(full("qx", 256), full("sx", 256), full("xin", 1024))
+    pick_u(0)
+
+    def split(src):
+        r = cores.index(src)
+        a, b = topo.engines(src, cores[(r + 1) % n]), topo.engines(src, cores[(r + n - 1) % n])
+        if len(a) <= len(b):
+            return a, [e for e in b if e not in a]
+        return [e for e in a if e not in b], b
+
+    e_up, e_down = split(core)
+    n_from = len(split(up)[1]) + len(split(down)[0])
+
+    def transfer(c, es, sem, views):
+        rid, pid, _s = topo.addr(c)
+        return RemoteDMATransfer(dst_ids=[DstId(rid=rid, pnc=pid)], dma_engine_mask=sum(1 << e for e in es), remote_sem=T.sem[sem],
+                                 srcs=[views[1]], dsts=[views[0]])
+
+    def send(to_up, to_down, reads, sem):
+        wait_for("g", needs("g", True, reads, []))
+        total["loc"] = total.get("loc", 0) + len(e_up) + len(e_down)
+        g.remote_dma_fused([transfer(up, e_up, sem, to_up), transfer(down, e_down, sem, to_down)], local_sem=T.sem.loc)
+        note("g", True, reads, [], {"sem": "loc", "cnt": total["loc"], "clk": dict(known["g"])})
+
+    def send_state(t):
+        q, s = reg("qx", t, 256), reg("sx", t, 256)
+        lo, hi = 2 * t, 2 * t + 1
+        send((u8(reg("lq", hi, 256)), u8(q)), (u8(reg("lq", lo, 256)), u8(q)), [q], "aq%d" % t)
+        send((ap(reg("lsc", hi, 256)), ap(s)), (ap(reg("lsc", lo, 256)), ap(s)), [s], "aq%d" % t)
+
+    for t in range(ROUNDS):
+        arrive("aq%d" % t, 2 * n_from, [reg("lq", t, 512), reg("lsc", t, 512)])
+        arrive("al%d" % t, n_from, [reg("lnd", t, 8)])
+
+    def score(t):
+        mm(4, reg("qp", t, 128), reg("sp", t, 128), reg("qx", t, 256), reg("sx", t, 256), 256)
+
+    def zreg(t, b, a, e):
+        return ("z", (4 * t + b) * ZW + a, (4 * t + b) * ZW + e)
+
+    def own_numbers(t, b):
+        z0 = zreg(t, b, 0, 256)
+        scopy(z0, ("ps", 512 * b, 512 * b + 256))
+        for k in (1, 2):
+            zk = zreg(t, b, 256 * k, 256 * k + 256)
+            dma("y", ap(zk), ap(z0), [zk], [z0], "zd%d" % (4 * t + b))
+
+    score(0)
+    send_state(0)
+
+    sc0, scs = new("fl", 768), new("fl", 128)
+    for k in range(3):
+        scan(blk(sc0, k), mask, sub(trn, k, 768, 3))
+    lists_first(0, sc0)
+
+    for t in range(ROUNDS):
+        last = t == ROUNDS - 1
+        pos, po = new("bl", 256), new("bl", 768)
+        sc_in = ("ps", 2048, 2304)
+        run("s", lambda: g.scalar.activation(ap(pos), ap(sc_in), AF.Sign, bias=-(2.0 ** -110)), [pos], [sc_in])
+        for k in range(3):
+            (vget if k == 2 else sget)(blk(po, k), pos, blk(ooff[t], k, 16))
+        if t == 0:
+            lists_rest(0, sc0)
+            scan(scs, sub(mask, 0, 128), sub(trn, 768, 896))
+            table(3, 7)
+            for k in range(3):
+                scopy(("m3", k, 768, 3), base, 0.0 if k else -1.0e29, 0.0)
+            for b in range(4):
+                quant(reg("qe", b, 128), reg("se", b, 128), reg("ec", b, 512))
+        for b in range(4):
+            mm(b, reg("qe", b, 128), reg("se", b, 128), reg("qx", t, 256), reg("sx", t, 256), 256)
+        spos, so = new("bl", 256), new("bl", 768)
+        scan(spos, mask, pos)
+        sv, so_g, svm = new("fl", 16), new("fl", 48), new("fl", 48)
+        ts(sv, sub(spos, 15, 256, 16), thr, A.is_ge, 0.5, A.subtract)
+        scan(blk(so, 2), mask, blk(po, 2))
+        for k in range(3):
+            tt(blk(svm, k, 16), blk(keys[t], k, 16), sv, A.mult)
+        for k in range(2):
+            scan(blk(so, k), mask, blk(po, k))
+        ts(so_g, sub(so, 15, 768, 16), thr, A.is_ge, 0.5, A.subtract)
+        pk = new("fl", 48)
+        tt(pk, so_g, svm, A.mult)
+        ra, rb, r = new("fl", 16), new("fl", 16), new("fl", 16)
+        tt(ra, blk(pk, 0, 16), blk(pk, 1, 16), A.min)
+        ts(rb, blk(pk, 2, 16), -0.0625, A.min)
+        tt(r, ra, rb, A.min)
+        m_i, m_o, k_i, oc_i, oc = new("il", 16), new("ul", 16), new("il", 16), new("il", 16), new("ul", 16)
+        ts(m_o, r, -0.0078125, A.mult)
+        ts(k_i, r, -4.0, A.mult)
+        ts(m_i, r, -0.0078125, A.mult)
+        rr, ro, rs, rd = new("fl", 256), new("fl", 256), new("fl", 256), new("fl", 16)
+        own_numbers(t, 0)
+        own_numbers(t, 1)
+        sget(rr, sub(ftab, 0, 1024), m_o)
+        ts(oc_i, k_i, 255, A.bitwise_and)
+        ts(rd, m_i, 1024.0, A.add, thr, A.mult)
+        vcopy(oc, oc_i)
+        sget(ro, rr, oc)
+        icx = new("fl", 64)
+        for i, k in enumerate([1, 2, 0, 1]):
+            tt(blk(icx, i, 16), blk(pk, k, 16), r, A.is_equal)
+        if t == 0:
+            for i in range(ROUNDS):
+                scopy(sub(fr[i], 768, 896), sub(base, 0, 128), 768.0)
+            decode(sub(toff[0], 48, 56), scs, 0, 128)
+            decode(sub(toff[0], 0, 48), sc0, 0, 768)
+            for k in range(3):
+                scopy(blk(nattab, k), base, float(k - 3072), 3.0)
+            scopy(sub(nattab, 768, 896), sub(base, 0, 128), -256.0)
+        ab, bb, dd = new("fl", 96), new("fl", 96), new("fl", 96)
+        for i in range(2):
+            tt(blk(ab, i, 48), c3 if i else fa[t], sub(icx, 16, 64), A.mult)
+            tt(blk(bb, i, 48), fb[t] if i else c2, sub(icx, 0, 48), A.mult)
+        tt(dd, ab, bb, A.add)
+        own_numbers(t, 2)
+        own_numbers(t, 3)
+        go = new("fl", 16)
+        scan(rs, mask, ro)
+        tt(go, sub(rs, 15, 256, 16), rd, A.is_equal)
+        dg, y, yo = new("fl", 96), new("il", 96), new("ul", 96)
+        for k in range(3):
+            tt(blk(dg, k, 16), blk(dd, k, 16), go, A.mult)
+        tt(sub(y, 0, 48), sub(dg, 0, 48), idg, A.add)
+        vcopy(sub(yo, 0, 48), sub(y, 0, 48))
+        f = fr[t]
+        for k in range(2):
+            sget(blk(f, k), ftab, blk(yo, k, 16))
+        for k in range(3, 6):
+            tt(blk(dg, k, 16), blk(dd, k, 16), go, A.mult)
+        tt(sub(y, 48, 96), sub(dg, 48, 96), idg, A.add)
+        vcopy(sub(yo, 48, 96), sub(y, 48, 96))
+        vget(blk(f, 2), ftab, blk(yo, 2, 16))
+        f1, nt = new("fl", 1024), new("fl", 896)
+        vget(sub(nt, 768, 896), f, sub(toff[t], 48, 56))
+        for k in range(2):
+            sget(blk(f1, k), f, blk(toff[t], k, 16))
+            if k == 0:
+                scopy(blk(f1, 3), blk(f1, 0))
+        ssc, s_i, s_c = new("fl", 128), new("il", 8), new("il", 8)
+        scan(ssc, sub(mask, 0, 128), sub(nt, 768, 896))
+        decode(s_i, ssc, 0, 128)
+        ts(s_c, s_i, 255, A.bitwise_and)
+        sd = new("snd", 8)
+        ts(sub(sd, 0, 4), sub(s_c, 0, 4), 256, A.add)
+        vcopy(sub(sd, 4, 8), sub(s_c, 4, 8))
+        send((ap(reg("lnd", 2 * t + 1, 4)), ap(sub(sd, 0, 4))), (ap(reg("lnd", 2 * t, 4)), ap(sub(sd, 4, 8))), [sd], "al%d" % t)
+        vget(blk(f1, 2), f, blk(toff[t], 2, 16))
+        for k in range(3):
+            (vget if k == 0 else sget)(blk(nt, k), f1, blk(yo, 3 + k, 16))
+        for b in range(4):
+            mm(4 + b, reg("qe", b, 128), reg("se", b, 128), reg("lq", t, 512), reg("lsc", t, 512), 512)
+        nsc = new("fl", 768)
+        for k in range(3):
+            scan(blk(nsc, k), mask, blk(nt, k))
+        x = toff[t + 1]
+        decode(sub(x, 0, 48), nsc, 0, 768)
+        for b in range(4):
+            (vcopy if b == 0 else scopy)(reg("nz", 4 * t + b, 512), reg("ps", 4 + b, 512))
+        if last:
+            quant(full("qv", 128), full("svp", 128), full("vin", 512))
+        else:
+            decode(sub(x, 48, 56), ssc, 0, 128)
+        for b in range(4):
+            (sget if b == 1 else vget)(zreg(t, b, 768, 896), reg("nz", 4 * t + b, 512), reg("lnd", t, 8))
+        tb = 1024 * t
+        for b in (0, 1):
+            ma, mb = reg("ma", 2 * t + b, 256), reg("mb", 2 * t + b, 256)
+            sget(ma, zreg(t, b, 0, 896), blk(x, 0, 16))
+            vmax(mb, zreg(t, b, 0, 896), blk(x, 1, 16), ma)
+            vmax(("mt", tb + b, tb + 1024, 4), zreg(t, b, 0, 896), blk(x, 2, 16), mb)
+        for b in (2, 3):
+            mg, ms = reg("mg", 2 * t + b - 2, 768), reg("ms", 2 * t + b - 2, 768)
+            for k in range(3):
+                sget(sub(mg, k, 768, 3), zreg(t, b, 0, 896), blk(x, k, 16))
+            scan(ms, full("m3", 768), mg, A.add, A.max)
+            vcopy(("mt", tb + b, tb + 1024, 4), sub(ms, 2, 768, 3))
+        quant(reg("qm", t, 256), reg("sm", t, 256), reg("mt", t, 1024))
+        if last:
+            otb, s_o = new("fl", 896), new("ul", 8)
+            decode(s_o, ssc, 0, 128)
+            for k in range(3):
+                sget(sub(otb, k, 768, 3), nattab, blk(x, k, 16))
+            sget(sub(otb, 768, 896), nattab, s_o)
+            dma("y", T.ot[:, :], T.fl[0:128:16, otb[1]:otb[2]], [], [otb], "out")
+        for b in range(4):
+            mm(4 + b, reg("qw", b, 128), reg("sw", b, 128), reg("qm", t, 256), reg("sm", t, 256), 256)
+        if not last:
+            if t == 0:
+                pick_u(1)
+            lists_first(t + 1, nsc)
+        for b in range(4):
+            tmp = reg("tm", b, 256)
+            wb = ("ps", 2048 + 512 * b, 2304 + 512 * b)
+            run("s", lambda: g.scalar.activation(ap(tmp), ap(wb), AF.Relu, scale=0.015625), [tmp], [wb])
+            tt(("xt", tb + b, tb + 1024, 4), tmp, ("ps", 512 * b, 512 * b + 256), A.add)
+        quant(reg("qx", t + 1, 256), reg("sx", t + 1, 256), reg("xt", t, 1024))
+        if not last:
+            score(t + 1)
+            send_state(t + 1)
+            if t == 0:
+                pick_u(2)
+            lists_rest(t + 1, nsc)
+
+    q, s = reg("qx", ROUNDS, 256), reg("sx", ROUNDS, 256)
+    mm(0, full("qv", 128), full("svp", 128), q, s, 256)
+    dma("y", T.oc[:, :], u8(q), [], [q], "out")
+    for k in range(4):
+        dma("y" if k % 2 else "s", T.osc[4 * k:4 * k + 4, :], T.sx[32 * k:32 * k + 4, s[1]:s[2]], [], [s], "out")
+    vcopy(full("yo", 256), ("ps", 0, 256))
+    dma("y", T.y[:, :], T.yo[:, :], [], [full("yo", 256)], "out")
+    for s in sorted(total):
+        if known["g"].get(s, 0) < total[s]:
+            g.wait_ge(T.sem[s], total[s])

@@ -2,7 +2,9 @@ from concourse.bass import DstId, RemoteDMATransfer
 from concourse.mybir import dt, AluOpType, ActivationFunctionType
 
 ROUNDS = 3
-ZW = 896
+ZW = 384
+QUARTER = 0.2499
+OPT = {}
 
 SCRATCH = {
     "xin": ("sbuf", [128, 1024], "bfloat16"),
@@ -12,15 +14,15 @@ SCRATCH = {
     "mt": ("sbuf", [128, 3072], "bfloat16"),
     "z": ("sbuf", [128, 12 * ZW], "bfloat16"),
     "nz": ("sbuf", [128, 12 * 512], "bfloat16"),
-    "ma": ("sbuf", [128, 1536], "bfloat16"),
-    "mb": ("sbuf", [128, 1536], "bfloat16"),
-    "mg": ("sbuf", [128, 4608], "bfloat16"),
-    "ms": ("sbuf", [128, 4608], "bfloat16"),
+    "ma": ("sbuf", [128, 12 * 256], "bfloat16"),
+    "mb": ("sbuf", [128, 12 * 256], "bfloat16"),
+    "mg": ("sbuf", [128, 6 * 768], "bfloat16"),
+    "ms": ("sbuf", [128, 6 * 768], "bfloat16"),
     "m3": ("sbuf", [128, 768], "bfloat16"),
     "tm": ("sbuf", [128, 1024], "float32"),
     "yo": ("sbuf", [128, 256], "float32"),
-    "ones": ("sbuf", [128, 512], "bfloat16"),
-    "ec": ("sbuf", [128, 2048], "bfloat16"),
+    "cb": ("sbuf", [128, 272], "float32"),
+    "ec": ("sbuf", [128, 528], "bfloat16"),
     "qe": ("sbuf", [128, 512], "float8_e4m3fn_x4"), "se": ("sbuf", [128, 512], "uint8"),
     "qu": ("sbuf", [128, 128], "float8_e4m3fn_x4"), "su": ("sbuf", [128, 128], "uint8"),
     "qp": ("sbuf", [128, 384], "float8_e4m3fn_x4"), "sp": ("sbuf", [128, 384], "uint8"),
@@ -30,15 +32,15 @@ SCRATCH = {
     "qm": ("sbuf", [128, 768], "float8_e4m3fn_x4"), "sm": ("sbuf", [128, 768], "uint8"),
     "lq": ("sbuf", [128, 1536], "float8_e4m3fn_x4"), "lsc": ("sbuf", [128, 1536], "uint8"),
     "twi": ("sbuf", [128, 56], "int32"),
-    "fl": ("sbuf", [128, 24000], "float32"),
-    "il": ("sbuf", [128, 1800], "int32"),
+    "fl": ("sbuf", [128, 22000], "float32"),
+    "il": ("sbuf", [128, 600], "int32"),
     "bl": ("sbuf", [128, 8800], "bfloat16"),
     "ul": ("sbuf", [128, 1800], "uint16"),
     "snd": ("sbuf", [128, 48], "uint16"),
     "lnd": ("sbuf", [128, 24], "uint16"),
     "ps": ("psum", [128, 4096], "float32"),
 }
-SEMAPHORES = (["sv", "ss", "st", "sg", "loc", "out"] + ["ld%d" % i for i in range(6)] + ["zd%d" % i for i in range(12)]
+SEMAPHORES = (["sv", "ss", "st", "sg", "loc", "out"] + ["ld%d" % i for i in range(6)]
               + ["aq%d" % t for t in range(3)] + ["al%d" % t for t in range(3)])
 
 
@@ -60,26 +62,24 @@ def rank_program(g, core, T, topo):
 
     def span(r):
         if r[0] == "ps":
-            return r[1] // 512 * 512, (r[2] + 511) // 512 * 512
-        return r[1], r[2]
+            return r[1] // 512 * 512, (r[2] + 511) // 512 * 512, 1
+        return r[1], r[2], (r[3] if len(r) > 3 else 1)
 
     def needs(q, dma, ins, outs):
         found = []
         for writing, regs in ((False, ins), (True, outs)):
             for r in regs:
-                a, b = span(r)
-                for (c, d, w, oq, odma, op) in touched.get(r[0], ()):
+                a, b, st = span(r)
+                for (c, d, st2, w, oq, odma, op) in touched.get(r[0], ()):
                     if c >= b or d <= a:
                         continue
-                    same = oq == q and not odma and not dma
+                    if st == st2 and st > 1 and (a - c) % st and not dma and not odma:
+                        continue
                     if r[0] == "ps":
-                        if same and (writing or not w):
+                        if oq == q and (writing or not w):
                             continue
-                    else:
-                        if not writing and not w:
-                            continue
-                        if same and writing:
-                            continue
+                    elif not writing and not w:
+                        continue
                     found.append(op)
         return found
 
@@ -108,8 +108,8 @@ def rank_program(g, core, T, topo):
     def note(q, dma, ins, outs, op):
         for w, regs in ((False, ins), (True, outs)):
             for r in regs:
-                a, b = span(r)
-                touched.setdefault(r[0], []).append((a, b, w, q, dma, op))
+                a, b, st = span(r)
+                touched.setdefault(r[0], []).append((a, b, st, w, q, dma, op))
 
     def run(q, fn, outs, ins):
         wait_for(q, needs(q, False, ins, outs))
@@ -181,7 +181,7 @@ def rank_program(g, core, T, topo):
     def fill(out, x):
         run("v", lambda: g.vector.memset(ap(out), x), [out], [])
 
-    def scan(out, d0, d1, op0=A.mult, op1=A.max):
+    def scan(out, d0, d1, op0=A.add, op1=A.max):
         run("v", lambda: g.vector.tensor_tensor_scan(ap(out), ap(d0), ap(d1), 0.0, op0, op1), [out], [d0, d1])
 
     def scopy(out, in0, bias=None, scale=1.0):
@@ -212,106 +212,91 @@ def rank_program(g, core, T, topo):
         out = ("ps", 512 * bank, 512 * bank + width)
         run("t", lambda: g.tensor.matmul_mx(ap(out), ap(w), ap(ws), ap(x), ap(xs), True, True), [out], [w, ws, x, xs])
 
+    get = {"v": vget, "s": sget}
+    copy = {"v": vcopy, "s": scopy}
+
     full = lambda name, w: (name, 0, w)
     dma("y", T.twi[:, :], T.tw[:, :], [full("twi", 56)], [], "ld0")
-    dma("s", T.xin[:, :], T.x[:, :], [full("xin", 1024)], [], "ld1")
-    dma("y", T.uin[:, :], T.u[:, :], [full("uin", 512)], [], "ld2")
-    dma("y", T.qw[:, :].bitcast(dt.uint8), T.wc[:, :], [full("qw", 512)], [], "ld3")
-    dma("y", T.sw[:, :], T.ws[:, :], [full("sw", 512)], [], "ld4")
-    dma("y", T.vin[:, :], T.v[:, :], [full("vin", 512)], [], "ld5")
+    dma("s", T.uin[:, :], T.u[:, :], [full("uin", 512)], [], "ld2")
+    dma("y", T.xin[:, :], T.x[:, :], [full("xin", 1024)], [], "ld1")
 
-    pcol = new("il", 1)
-    jrow = new("bl", 128)
-    base = new("fl", 256)
-    uo_i, id_i, nat_i = new("il", 24), new("il", 48), new("il", 48)
+    base, pf = ("cb", 0, 256), ("cb", 256, 257)
+    pcol, uo_i, id_i = new("il", 1), new("il", 24), new("il", 48)
+    jrow = new("bl", 256)
+    iota(base, [[1, 256]], 0, 0, True)
     iota(pcol, [[0, 1]], 0, 1)
-    iota(jrow, [[0, 8], [1, 16]], 0, 0, True)
-    iota(base, [[1, 256]], 1024, 0, True)
+    iota(jrow, [[0, 16], [1, 16]], 0, 0, True)
     iota(uo_i, [[1, 3], [16, 8]], 0, 0)
-    iota(id_i, [[256, 3], [16, 16]], 0, 0)
-    iota(nat_i, [[1, 3], [48, 16]], 0, 0)
-    fill(full("ones", 512), 1.0)
-    for b in range(4):
-        e = reg("ec", b, 512)
-        run("g", lambda: g.affine_select(ap(e), T.ones[:, :], [[1, 512]], A.is_equal, 0.0, -b, -4), [e], [full("ones", 512)])
+    iota(id_i, [[1, 3], [64, 16]], 0, 0)
+    iota(pf, [[0, 1]], 0, 1, True)
 
-    icol_i, icol = new("il", 1), new("fl", 1)
+    fill(full("ec", 528), 0.0)
+    pos = new("bl", 384)
+    fill(sub(pos, 256, 384), 1024.0)
+    gz = new("fl", 192)
+    dy = new("fl", 144)
+    fill(gz, 0.0)
+    fill(dy, 1024.0)
+    natinv = new("fl", 896)
+    for k in range(2):
+        scopy(sub(natinv, k, 768, 3), base, float(k), 4.0)
+    scopy(sub(natinv, 768, 896), sub(base, 0, 128), 1025.0, 4.0)
+    ts(sub(natinv, 2, 768, 3), base, 4.0, A.mult, 2.0, A.add)
+    tab, f, ntn, nattab = new("fl", 2048), new("fl", 1536), new("fl", 1024), new("fl", 1536)
+
+    def before(a, b):
+        for k in range(a, b):
+            scopy(sub(tab, 1024 + k, 2048, 4), base, float((k + 2) % 3), 4.0)
+    th = OPT.get("th", 3)
+    before(0, th)
+
+    icol_i, icol, cq, cols, ic4 = new("il", 1), new("fl", 1), new("fl", 1), new("fl", 3), new("fl", 1)
+    cpm, cp, cps = sub(cols, 0, 1), sub(cols, 1, 2), sub(cols, 2, 3)
     ts(icol_i, pcol, 15, A.bitwise_and)
     vcopy(icol, icol_i)
-    mask = new("bl", 256)
-    ts(sub(mask, 0, 128), jrow, icol, A.is_gt, 2.0, A.mult)
-    half, hit, one = new("fl", 16), new("fl", 16), new("fl", 16)
-    fill(half, 0.5)
-    fill(one, 1.0)
-    ts(hit, sub(jrow, 0, 16), icol, A.is_equal)
-    vcopy(sub(mask, 128, 256), sub(mask, 0, 128))
-    dsc_r, thr_r = new("fl", 16), new("fl", 16)
-    scan(dsc_r, half, hit, A.mult, A.add)
-    scan(thr_r, sub(mask, 0, 16), one)
-    dsc, thr = sub(dsc_r, 15, 16), sub(thr_r, 15, 16)
-
-    natinv = new("fl", 896)
-    for k in range(3):
-        ts(sub(natinv, k, 768, 3), base, 256.0 * k, A.add)
-    ts(sub(natinv, 768, 896), sub(base, 0, 128), 768.0, A.add)
-    ftab, nattab = new("fl", 1792), new("fl", 896)
-    fr = [new("fl", 896) for t in range(ROUNDS)]
-
-    def table(a, b):
-        for i in range(a, b):
-            scopy(blk(ftab, i), base, float([0, 256, 512, 768, 512, 0, 256][i]))
-    table(0, 3)
+    ts(cq, icol_i, -4096.0, A.mult)
+    ts(ic4, icol_i, 4.0, A.mult)
+    mk, mask = new("bl", 256), new("bl", 256)
+    ts(mk, jrow, icol, A.is_gt, 135168.0, A.mult)
+    ts(cols, sub(base, 59, 62), 1024.0, A.mult, cq, A.add)
+    ts(mask, mk, -131072.0, A.add)
+    ids = sub(dy, 2, 144, 3)
+    own, c1 = new("fl", 48), new("fl", 48)
+    uo = new("ul", 24)
+    vcopy(uo, uo_i)
+    ts(ids, id_i, ic4, A.add)
 
     trn = new("fl", 896)
-    tw_o = new("ul", 56)
+    tw_o, x0 = new("ul", 56), new("ul", 48)
     vcopy(tw_o, full("twi", 56))
-    sget(trn, natinv, tw_o)
-    uo, idg, ic3 = new("ul", 24), new("il", 48), new("fl", 1)
-    own_a, own, c1, c2, c3, c4 = [new("fl", 48) for i in range(6)]
-    vcopy(uo, uo_i)
-    ts(idg, id_i, icol, A.add)
-    ts(ic3, icol, 3.0, A.mult)
-    ts(own_a, nat_i, -1.0, A.mult, 1023.0, A.add)
-    fill(sub(c2, 0, 16), 512.0)
-    fill(sub(c2, 16, 48), -256.0)
-    ts(own, own_a, ic3, A.subtract)
-    ts(c1, idg, -1.0, A.mult, 1024.0, A.add)
-    fill(sub(c3, 0, 32), 256.0)
-    fill(sub(c3, 32, 48), -512.0)
-    ts(c4, idg, -1.0, A.mult, 256.0, A.add)
+    cut = OPT.get("cut", 40)
+    sget(sub(trn, 0, 16 * cut), natinv, sub(tw_o, 0, cut))
+    vget(sub(trn, 16 * cut, 896), natinv, sub(tw_o, cut, 56))
+    ts(x0, full("twi", 48), -1.0, A.add, 1.0 / 3.0, A.mult)
+    ts(own, ids, -8192.0, A.mult, 8192.0 * 1023, A.add)
+    ts(c1, ids, -1.0, A.mult, 1024.0, A.add)
+    ts(("ec", 3, 515, 4), sub(base, 0, 128), pf, A.is_equal)
 
-    tix = [new("il", 80) for t in range(ROUNDS)]
-    toff = [new("ul", 64) for t in range(ROUNDS + 1)]
-    fa, fb = [new("fl", 48) for t in range(ROUNDS)], [new("fl", 48) for t in range(ROUNDS)]
-    keys = [new("fl", 48) for t in range(ROUNDS)]
-    ooff = [new("ul", 48) for t in range(ROUNDS)]
-    oth = [new("il", 48) for t in range(ROUNDS)]
+    dx = [new("fl", 240) for t in range(ROUNDS)]
+    fa, fb, keys = [[new("fl", 48) for t in range(ROUNDS)] for i in range(3)]
+    xs = [x0] + [new("ul", 48) for t in range(ROUNDS)]
+    toffs = [new("ul", 8) for t in range(ROUNDS + 1)]
 
-    def decode(out, sc, a, b):
-        ts(out, sub(sc, a + 15, b, 16), dsc, A.mult, 1024.0, A.subtract)
+    def ends(sc, a, b):
+        return sub(sc, a + 15, b, 16)
 
-    def lists_first(t, sc):
-        own_t = sub(tix[t], 0, 48)
-        decode(own_t, sc, 0, 768)
-        ts(oth[t], own_t, 255, A.bitwise_and)
-        vcopy(ooff[t], oth[t])
-
-    def lists_rest(t, sc):
-        ti, o = tix[t], oth[t]
-        own_t = sub(ti, 0, 48)
-        hi = new("il", 48)
-        n1, n2, lt, n3, n4, o1 = [new("fl", 48) for i in range(6)]
-        ts(hi, own_t, 8, A.logical_shift_right)
-        ts(n1, o, -3.0, A.mult, 1023.0, A.add)
-        ts(lt, own_t, 768.0, A.is_lt, 512.0, A.mult)
-        ts(o1, o, 0.001953125, A.mult)
-        tt(n2, n1, hi, A.subtract)
-        decode(sub(ti, 48, 80), sc, 0, 512)
-        tt(n3, n2, own, A.max)
-        tt(fb[t], sub(ti, 16, 64), c4, A.add)
-        tt(n4, n3, o1, A.add)
-        tt(fa[t], sub(ti, 32, 80), c1, A.add)
-        tt(keys[t], n4, lt, A.mult)
+    def lists(t, sc, ssc):
+        d = dx[t]
+        n1, mx = new("fl", 48), new("fl", 48)
+        tw = sub(d, 2, 144, 3)
+        return [lambda: ts(tw, ends(sc, 0, 768), cp, A.subtract),
+                lambda: ts(sub(d, 146, 240, 3), ends(sc, 0, 512), cp, A.subtract),
+                lambda: ts(n1, tw, -8192.0, A.mult, 8192.0 * 1023, A.add),
+                lambda: ts(toffs[t], ends(ssc, 0, 128), cp, A.subtract),
+                lambda: tt(mx, n1, own, A.max),
+                lambda: tt(fa[t], sub(d, 98, 240, 3), c1, A.add),
+                lambda: tt(keys[t], mx, tw, A.add),
+                lambda: tt(fb[t], sub(d, 50, 192, 3), tw, A.subtract)]
 
     def pick_u(t):
         off = blk(uo, t, 8)
@@ -320,9 +305,19 @@ def rank_program(g, core, T, topo):
             [("qp", c, d)], [("qu", 0, 128), uo])
         run("s", lambda: g.scalar.activation(T.sp[:, c:d], T.su[:, 0:128].indirect(ap(off)), AF.Copy), [("sp", c, d)], [("su", 0, 128), uo])
 
+    sc0, scs = new("fl", 768), new("fl", 128)
+    packs = [(lambda b: lambda: quant(reg("qe", b, 128), reg("se", b, 128), ("ec", 3 - b, 515 - b)))(b) for b in range(4)]
+    scans = [(lambda k: lambda: scan(blk(sc0, k), mask, sub(trn, k, 768, 3)))(k) for k in range(3)]
+    scans.append(lambda: scan(scs, sub(mask, 0, 128), sub(trn, 768, 896)))
+    first = packs + scans + lists(0, sc0, scs)
+    n1, n2 = OPT.get("n1", 4), OPT.get("n2", 6)
+    for c in first[:n1]:
+        c()
     quant(full("qu", 128), full("su", 128), full("uin", 512))
-    quant(full("qx", 256), full("sx", 256), full("xin", 1024))
     pick_u(0)
+    quant(full("qx", 256), full("sx", 256), full("xin", 1024))
+    dma("y", T.qw[:, :].bitcast(dt.uint8), T.wc[:, :], [full("qw", 512)], [], "ld3")
+    dma("y", T.sw[:, :], T.ws[:, :], [full("sw", 512)], [], "ld4")
 
     def split(src):
         r = cores.index(src)
@@ -361,158 +356,172 @@ def rank_program(g, core, T, topo):
     def zreg(t, b, a, e):
         return ("z", (4 * t + b) * ZW + a, (4 * t + b) * ZW + e)
 
-    def own_numbers(t, b):
-        z0 = zreg(t, b, 0, 256)
-        scopy(z0, ("ps", 512 * b, 512 * b + 256))
-        for k in (1, 2):
-            zk = zreg(t, b, 256 * k, 256 * k + 256)
-            dma("y", ap(zk), ap(z0), [zk], [z0], "zd%d" % (4 * t + b))
-
     score(0)
     send_state(0)
-
-    sc0, scs = new("fl", 768), new("fl", 128)
+    iota(sub(tab, 0, 1024), [[1, 1024]], 0, 0, True)
+    iota(sub(f, 1024, 1536), [[1, 512]], 1024, 0, True)
     for k in range(3):
-        scan(blk(sc0, k), mask, sub(trn, k, 768, 3))
-    lists_first(0, sc0)
+        scopy(sub(ntn, (k + 2) % 3, 1024, 4), sub(trn, k, 768, 3))
+
+    nsc = sc0
+    for c in first[n1:n2]:
+        c()
 
     for t in range(ROUNDS):
         last = t == ROUNDS - 1
-        pos, po = new("bl", 256), new("bl", 768)
-        sc_in = ("ps", 2048, 2304)
-        run("s", lambda: g.scalar.activation(ap(pos), ap(sc_in), AF.Sign, bias=-(2.0 ** -110)), [pos], [sc_in])
-        for k in range(3):
-            (vget if k == 2 else sget)(blk(po, k), pos, blk(ooff[t], k, 16))
+        po = new("bl", 768)
+        ts(sub(pos, 0, 256), ("ps", 2048, 2304), 0.0, A.is_gt, 2048.0, A.mult)
         if t == 0:
-            lists_rest(0, sc0)
-            scan(scs, sub(mask, 0, 128), sub(trn, 768, 896))
-            table(3, 7)
+            part = [sub(po, k, 768, 3) for k in range(3)]
+            sget(po, pos, xs[0])
+            for c in first[n2:]:
+                c()
+        else:
+            part = [blk(po, k) for k in range(3)]
             for k in range(3):
-                scopy(("m3", k, 768, 3), base, 0.0 if k else -1.0e29, 0.0)
-            for b in range(4):
-                quant(reg("qe", b, 128), reg("se", b, 128), reg("ec", b, 512))
+                get["ssv"[k]](part[k], pos, blk(xs[t], k, 16))
         for b in range(4):
             mm(b, reg("qe", b, 128), reg("se", b, 128), reg("qx", t, 256), reg("sx", t, 256), 256)
         spos, so = new("bl", 256), new("bl", 768)
-        scan(spos, mask, pos)
+        scan(spos, mask, sub(pos, 0, 256))
         sv, so_g, svm = new("fl", 16), new("fl", 48), new("fl", 48)
-        ts(sv, sub(spos, 15, 256, 16), thr, A.is_ge, 0.5, A.subtract)
-        scan(blk(so, 2), mask, blk(po, 2))
+        ts(sv, ends(spos, 0, 256), cps, A.subtract, -1.0 / 1024, A.mult)
+        if t:
+            scan(blk(so, 0), mask, part[0])
         for k in range(3):
             tt(blk(svm, k, 16), blk(keys[t], k, 16), sv, A.mult)
-        for k in range(2):
-            scan(blk(so, k), mask, blk(po, k))
-        ts(so_g, sub(so, 15, 768, 16), thr, A.is_ge, 0.5, A.subtract)
+        for k in ((2, 1) if t else (0, 1, 2)):
+            scan(blk(so, k), mask, part[k])
+        ts(so_g, ends(so, 0, 768), cps, A.subtract, 1.0 / 1024, A.mult)
+        if t == 0:
+            scopy(sub(ntn, 3, 1024, 4), base)
+            scopy(sub(f, 3, 1024, 4), base)
+            before(th, 4)
+        for b in range(4):
+            scopy(zreg(t, b, 0, 256), ("ps", 512 * b, 512 * b + 256))
         pk = new("fl", 48)
         tt(pk, so_g, svm, A.mult)
-        ra, rb, r = new("fl", 16), new("fl", 16), new("fl", 16)
-        tt(ra, blk(pk, 0, 16), blk(pk, 1, 16), A.min)
-        ts(rb, blk(pk, 2, 16), -0.0625, A.min)
-        tt(r, ra, rb, A.min)
-        m_i, m_o, k_i, oc_i, oc = new("il", 16), new("ul", 16), new("il", 16), new("il", 16), new("ul", 16)
-        ts(m_o, r, -0.0078125, A.mult)
-        ts(k_i, r, -4.0, A.mult)
-        ts(m_i, r, -0.0078125, A.mult)
-        rr, ro, rs, rd = new("fl", 256), new("fl", 256), new("fl", 256), new("fl", 16)
-        own_numbers(t, 0)
-        own_numbers(t, 1)
-        sget(rr, sub(ftab, 0, 1024), m_o)
-        ts(oc_i, k_i, 255, A.bitwise_and)
-        ts(rd, m_i, 1024.0, A.add, thr, A.mult)
-        vcopy(oc, oc_i)
+        ra, rb, r = new("fl", 16), new("fl", 16), new("il", 16)
+        tt(ra, blk(pk, 0, 16), blk(pk, 1, 16), A.max)
+        ts(rb, blk(pk, 2, 16), 1.0, A.max)
+        tt(r, ra, rb, A.max)
+        m_o, c_i, oc, cn, rd = new("ul", 16), new("il", 16), new("ul", 16), new("ul", 16), new("fl", 16)
+        ts(m_o, r, 1.0 / 8192, A.mult)
+        ts(c_i, r, 2047, A.bitwise_and)
+        rr, ro, rs, tq, tqs = [new("fl", 256) for i in range(5)]
+        sget(rr, sub(tab, 0, 1024), m_o)
+        icx = [sub(gz, 48 * i + 1, 48 * i + 48, 3) for i in range(4)]
+        tt(icx[0], blk(pk, 1, 16), r, A.is_equal)
+        ts(oc, c_i, QUARTER, A.mult)
+        vcopy(cn, c_i)
         sget(ro, rr, oc)
-        icx = new("fl", 64)
-        for i, k in enumerate([1, 2, 0, 1]):
-            tt(blk(icx, i, 16), blk(pk, k, 16), r, A.is_equal)
-        if t == 0:
-            for i in range(ROUNDS):
-                scopy(sub(fr[i], 768, 896), sub(base, 0, 128), 768.0)
-            decode(sub(toff[0], 48, 56), scs, 0, 128)
-            decode(sub(toff[0], 0, 48), sc0, 0, 768)
-            for k in range(3):
-                scopy(blk(nattab, k), base, float(k - 3072), 3.0)
-            scopy(sub(nattab, 768, 896), sub(base, 0, 128), -256.0)
-        ab, bb, dd = new("fl", 96), new("fl", 96), new("fl", 96)
-        for i in range(2):
-            tt(blk(ab, i, 48), c3 if i else fa[t], sub(icx, 16, 64), A.mult)
-            tt(blk(bb, i, 48), fb[t] if i else c2, sub(icx, 0, 48), A.mult)
-        tt(dd, ab, bb, A.add)
-        own_numbers(t, 2)
-        own_numbers(t, 3)
-        go = new("fl", 16)
-        scan(rs, mask, ro)
-        tt(go, sub(rs, 15, 256, 16), rd, A.is_equal)
-        dg, y, yo = new("fl", 96), new("il", 96), new("ul", 96)
-        for k in range(3):
-            tt(blk(dg, k, 16), blk(dd, k, 16), go, A.mult)
-        tt(sub(y, 0, 48), sub(dg, 0, 48), idg, A.add)
-        vcopy(sub(yo, 0, 48), sub(y, 0, 48))
-        f = fr[t]
-        for k in range(2):
-            sget(blk(f, k), ftab, blk(yo, k, 16))
-        for k in range(3, 6):
-            tt(blk(dg, k, 16), blk(dd, k, 16), go, A.mult)
-        tt(sub(y, 48, 96), sub(dg, 48, 96), idg, A.add)
-        vcopy(sub(yo, 48, 96), sub(y, 48, 96))
-        vget(blk(f, 2), ftab, blk(yo, 2, 16))
-        f1, nt = new("fl", 1024), new("fl", 896)
-        vget(sub(nt, 768, 896), f, sub(toff[t], 48, 56))
-        for k in range(2):
-            sget(blk(f1, k), f, blk(toff[t], k, 16))
-            if k == 0:
-                scopy(blk(f1, 3), blk(f1, 0))
-        ssc, s_i, s_c = new("fl", 128), new("il", 8), new("il", 8)
-        scan(ssc, sub(mask, 0, 128), sub(nt, 768, 896))
-        decode(s_i, ssc, 0, 128)
-        ts(s_c, s_i, 255, A.bitwise_and)
-        sd = new("snd", 8)
-        ts(sub(sd, 0, 4), sub(s_c, 0, 4), 256, A.add)
-        vcopy(sub(sd, 4, 8), sub(s_c, 4, 8))
-        send((ap(reg("lnd", 2 * t + 1, 4)), ap(sub(sd, 0, 4))), (ap(reg("lnd", 2 * t, 4)), ap(sub(sd, 4, 8))), [sd], "al%d" % t)
-        vget(blk(f1, 2), f, blk(toff[t], 2, 16))
-        for k in range(3):
-            (vget if k == 0 else sget)(blk(nt, k), f1, blk(yo, 3 + k, 16))
+        sget(tq, ntn, cn)
+        for i, k in ((1, 2), (2, 0), (3, 1)):
+            tt(icx[i], blk(pk, k, 16), r, A.is_equal)
+        ts(rd, m_o, cp, A.add)
+        ia = sub(gz, 49, 192, 3)
+        tt(sub(dy, 1, 144, 3), fa[t], ia, A.mult)
+        tt(sub(dx[t], 1, 144, 3), fb[t], ia, A.mult)
         for b in range(4):
             mm(4 + b, reg("qe", b, 128), reg("se", b, 128), reg("lq", t, 512), reg("lsc", t, 512), 512)
+        todo = [0, 1, 2, 3]
+
+        def unpack(q, cnt):
+            for i in range(cnt):
+                b = todo.pop(0)
+                copy[q](reg("nz", 4 * t + b, 512), reg("ps", 4 + b, 512))
+        unpack("s", OPT.get("nz1", 0) if t else 0)
+        ys, yo, xx, xo = new("fl", 144), new("ul", 48), new("fl", 144), new("ul", 48)
+        scan(rs, mask, ro)
+        for k in range(3):
+            tt(sub(gz, 48 * k + 2, 48 * k + 48, 3), ends(rs, 0, 256), rd, A.is_equal)
+        scan(ys, sub(gz, 0, 144), dy, A.mult, A.add)
+        vcopy(yo, sub(ys, 2, 144, 3))
+        nf = OPT.get("nf", 40)
+
+        def expand(q, a, b):
+            while a < b:
+                k, e = a // 16, min(b, a // 16 * 16 + 16)
+                get[q](sub(f, k + 64 * (a - 16 * k), 64 * (e - 16 * k), 4), tab, sub(yo, a, e))
+                a = e
+        expand("s", 0, nf)
+        scan(tqs, mask, tq)
+        for k in range(3):
+            tt(sub(dx[t], 48 * k, 48 * k + 48, 3), ends(tqs, 0, 256), ends(nsc, 256 * k, 256 * k + 256), A.subtract)
+        scan(xx, sub(gz, 0, 144), sub(dx[t], 0, 144), A.mult, A.add)
+        vcopy(xo, sub(xx, 2, 144, 3))
+        expand("v", nf, 48)
+        nts, ssc, sd = new("fl", 128), new("fl", 128), new("snd", 8)
+        vget(nts, f, toffs[t])
+        nn = OPT.get("nn", 2)
+        for k in range(nn):
+            sget(sub(ntn, (k + 2) % 3, 1024, 4), f, blk(xo, k, 16))
+        scan(ssc, sub(mask, 0, 128), nts)
+        ts(sub(sd, 0, 4), ends(ssc, 0, 64), cpm, A.subtract, QUARTER, A.mult)
+        ts(sub(sd, 4, 8), ends(ssc, 64, 128), cp, A.subtract, QUARTER, A.mult)
+        send((ap(reg("lnd", 2 * t + 1, 4)), ap(sub(sd, 0, 4))), (ap(reg("lnd", 2 * t, 4)), ap(sub(sd, 4, 8))), [sd], "al%d" % t)
+        if t == 0:
+            iota(sub(nattab, 0, 1024), [[3, 256], [1, 4]], 0, 0, True)
+        if t == 1:
+            iota(sub(nattab, 1024, 1536), [[1, 128], [0, 4]], 768, 0, True)
+        for k in range(nn, 3):
+            vget(sub(ntn, (k + 2) % 3, 1024, 4), f, blk(xo, k, 16))
         nsc = new("fl", 768)
         for k in range(3):
-            scan(blk(nsc, k), mask, blk(nt, k))
-        x = toff[t + 1]
-        decode(sub(x, 0, 48), nsc, 0, 768)
-        for b in range(4):
-            (vcopy if b == 0 else scopy)(reg("nz", 4 * t + b, 512), reg("ps", 4 + b, 512))
+            scan(blk(nsc, k), mask, sub(ntn, (k + 2) % 3, 1024, 4))
+        x = xs[t + 1]
+        ts(x, ends(nsc, 0, 768), cp, A.subtract, QUARTER, A.mult)
+        if t == 0:
+            dma("y", T.vin[:, :], T.v[:, :], [full("vin", 512)], [nsc], "ld5")
+            for k in range(3):
+                ts(("m3", k, 768, 3), jrow, 0.0, A.mult, 0.0 if k else -1.0e29, A.add)
+        nv = OPT.get("nzv", 0)
+        unpack("s", len(todo) - nv)
+        g1 = OPT.get("gap1", 4)
         if last:
-            quant(full("qv", 128), full("svp", 128), full("vin", 512))
+            cl, s_o, otb = new("ul", 48), new("ul", 8), new("fl", 896)
+            later = [lambda: ts(cl, ends(nsc, 0, 768), cp, A.subtract), lambda: ts(s_o, ends(ssc, 0, 128), cp, A.subtract),
+                     lambda: quant(full("qv", 128), full("svp", 128), full("vin", 512)),
+                     lambda: vget(sub(otb, 0, 768, 3), nattab, blk(cl, 0, 16)),
+                     lambda: vget(sub(otb, 1, 768, 3), nattab, blk(cl, 1, 16))]
+            g1 = OPT.get("gapl", 4)
         else:
-            decode(sub(x, 48, 56), ssc, 0, 128)
-        for b in range(4):
-            (sget if b == 1 else vget)(zreg(t, b, 768, 896), reg("nz", 4 * t + b, 512), reg("lnd", t, 8))
+            later = lists(t + 1, nsc, ssc)
+        for c in later[:g1]:
+            c()
+        unpack("v", nv)
         tb = 1024 * t
-        for b in (0, 1):
-            ma, mb = reg("ma", 2 * t + b, 256), reg("mb", 2 * t + b, 256)
-            sget(ma, zreg(t, b, 0, 896), blk(x, 0, 16))
-            vmax(mb, zreg(t, b, 0, 896), blk(x, 1, 16), ma)
-            vmax(("mt", tb + b, tb + 1024, 4), zreg(t, b, 0, 896), blk(x, 2, 16), mb)
-        for b in (2, 3):
-            mg, ms = reg("mg", 2 * t + b - 2, 768), reg("ms", 2 * t + b - 2, 768)
+        win = [zreg(t, b, 0, ZW) for b in range(4)]
+        outs = [("mt", tb + b, tb + 1024, 4) for b in range(4)]
+        ma, mb = [reg("ma", 4 * t + b, 256) for b in range(4)], [reg("mb", 4 * t + b, 256) for b in range(4)]
+        mg, ms = [reg("mg", 2 * t + b % 2, 768) for b in range(4)], [reg("ms", 2 * t + b % 2, 768) for b in range(4)]
+
+        def side_by_side(b):
             for k in range(3):
-                sget(sub(mg, k, 768, 3), zreg(t, b, 0, 896), blk(x, k, 16))
-            scan(ms, full("m3", 768), mg, A.add, A.max)
-            vcopy(("mt", tb + b, tb + 1024, 4), sub(ms, 2, 768, 3))
+                sget(sub(mg[b], k, 768, 3), win[b], blk(x, k, 16))
+        steps = {"B": lambda b: vget(zreg(t, b, 256, 384), reg("nz", 4 * t + b, 512), reg("lnd", t, 8)),
+                 "b": lambda b: sget(zreg(t, b, 256, 384), reg("nz", 4 * t + b, 512), reg("lnd", t, 8)),
+                 "G": lambda b: vget(ma[b], win[b], blk(x, 0, 16)),
+                 "g": lambda b: sget(ma[b], win[b], blk(x, 0, 16)),
+                 "M": lambda b: vmax(mb[b], win[b], blk(x, 1, 16), ma[b]),
+                 "O": lambda b: vmax(outs[b], win[b], blk(x, 2, 16), mb[b]),
+                 "s": side_by_side,
+                 "R": lambda b: scan(ms[b], full("m3", 768), mg[b]),
+                 "C": lambda b: vcopy(outs[b], sub(ms[b], 2, 768, 3))}
+        for step in OPT.get("morder", "b2 B0 g2 B1 b3 G0 g1 M2 M0 s3 O2 M1 O0 R3 O1 C3").split():
+            steps[step[0]](int(step[1]))
         quant(reg("qm", t, 256), reg("sm", t, 256), reg("mt", t, 1024))
-        if last:
-            otb, s_o = new("fl", 896), new("ul", 8)
-            decode(s_o, ssc, 0, 128)
-            for k in range(3):
-                sget(sub(otb, k, 768, 3), nattab, blk(x, k, 16))
-            sget(sub(otb, 768, 896), nattab, s_o)
-            dma("y", T.ot[:, :], T.fl[0:128:16, otb[1]:otb[2]], [], [otb], "out")
         for b in range(4):
             mm(4 + b, reg("qw", b, 128), reg("sw", b, 128), reg("qm", t, 256), reg("sm", t, 256), 256)
-        if not last:
-            if t == 0:
-                pick_u(1)
-            lists_first(t + 1, nsc)
+        for c in later[g1:]:
+            c()
+        if t == 0:
+            pick_u(1)
+            pick_u(2)
+        if last:
+            sget(sub(otb, 2, 768, 3), nattab, blk(cl, 2, 16))
+            sget(sub(otb, 768, 896), nattab, s_o)
+            dma("y", T.ot[:, :], T.fl[0:128:16, otb[1]:otb[2]], [], [otb], "out")
         for b in range(4):
             tmp = reg("tm", b, 256)
             wb = ("ps", 2048 + 512 * b, 2304 + 512 * b)
@@ -522,9 +531,6 @@ def rank_program(g, core, T, topo):
         if not last:
             score(t + 1)
             send_state(t + 1)
-            if t == 0:
-                pick_u(2)
-            lists_rest(t + 1, nsc)
 
     q, s = reg("qx", ROUNDS, 256), reg("sx", ROUNDS, 256)
     mm(0, full("qv", 128), full("svp", 128), q, s, 256)

@@ -5,6 +5,8 @@ ROUNDS = 3
 ZW = 384
 QUARTER = 0.2499
 OPT = {}
+H = OPT.get("H", 2)
+HW = 256 // H
 
 SCRATCH = {
     "xin": ("sbuf", [128, 1024], "bfloat16"),
@@ -21,7 +23,7 @@ SCRATCH = {
     "m3": ("sbuf", [128, 768], "bfloat16"),
     "tm": ("sbuf", [128, 1024], "float32"),
     "yo": ("sbuf", [128, 256], "float32"),
-    "cb": ("sbuf", [128, 272], "float32"),
+    "cb": ("sbuf", [128, 400], "float32"),
     "ec": ("sbuf", [128, 528], "bfloat16"),
     "qe": ("sbuf", [128, 512], "float8_e4m3fn_x4"), "se": ("sbuf", [128, 512], "uint8"),
     "qu": ("sbuf", [128, 128], "float8_e4m3fn_x4"), "su": ("sbuf", [128, 128], "uint8"),
@@ -32,10 +34,11 @@ SCRATCH = {
     "qm": ("sbuf", [128, 768], "float8_e4m3fn_x4"), "sm": ("sbuf", [128, 768], "uint8"),
     "lq": ("sbuf", [128, 1536], "float8_e4m3fn_x4"), "lsc": ("sbuf", [128, 1536], "uint8"),
     "twi": ("sbuf", [128, 56], "int32"),
-    "fl": ("sbuf", [128, 22000], "float32"),
+    "fl": ("sbuf", [128, 11000], "float32"),
     "il": ("sbuf", [128, 600], "int32"),
-    "bl": ("sbuf", [128, 8800], "bfloat16"),
+    "bl": ("sbuf", [128, 384], "bfloat16"),
     "ul": ("sbuf", [128, 1800], "uint16"),
+    "hl": ("sbuf", [128, 20000], "float16"),
     "snd": ("sbuf", [128, 48], "uint16"),
     "lnd": ("sbuf", [128, 24], "uint16"),
     "ps": ("psum", [128, 4096], "float32"),
@@ -138,7 +141,7 @@ def rank_program(g, core, T, topo):
     def u8(r):
         return ap(r).bitcast(dt.uint8)
 
-    unit = {"fl": 16, "il": 16, "bl": 32, "ul": 32, "snd": 16}
+    unit = {"fl": 16, "il": 16, "bl": 32, "hl": 32, "ul": 32, "snd": 16}
     free = {b: 0 for b in unit}
 
     def new(buf, w):
@@ -222,81 +225,54 @@ def rank_program(g, core, T, topo):
 
     base, pf = ("cb", 0, 256), ("cb", 256, 257)
     pcol, uo_i, id_i = new("il", 1), new("il", 24), new("il", 48)
-    jrow = new("bl", 256)
+    jrow = new("hl", 128)
     iota(base, [[1, 256]], 0, 0, True)
     iota(pcol, [[0, 1]], 0, 1)
-    iota(jrow, [[0, 16], [1, 16]], 0, 0, True)
     iota(uo_i, [[1, 3], [16, 8]], 0, 0)
+    iota(("cb", 272, 400), [[0, 8], [1, 16]], -1, 0, True)
     iota(id_i, [[1, 3], [64, 16]], 0, 0)
     iota(pf, [[0, 1]], 0, 1, True)
+    jrow = ("cb", 272, 400)
 
-    fill(full("ec", 528), 0.0)
     pos = new("bl", 384)
-    fill(sub(pos, 256, 384), 1024.0)
-    gz = new("fl", 192)
-    dy = new("fl", 144)
-    fill(gz, 0.0)
-    fill(dy, 1024.0)
+    gz = new("hl", 192)
+    dy = new("hl", 144)
+    keep = new("fl", 48)
     natinv = new("fl", 896)
-    for k in range(2):
-        scopy(sub(natinv, k, 768, 3), base, float(k), 4.0)
-    scopy(sub(natinv, 768, 896), sub(base, 0, 128), 1025.0, 4.0)
-    ts(sub(natinv, 2, 768, 3), base, 4.0, A.mult, 2.0, A.add)
     tab, f, ntn, nattab = new("fl", 2048), new("fl", 1536), new("fl", 1024), new("fl", 1536)
-
-    def before(a, b):
-        for k in range(a, b):
-            scopy(sub(tab, 1024 + k, 2048, 4), base, float((k + 2) % 3), 4.0)
-    th = OPT.get("th", 3)
-    before(0, th)
-
-    icol_i, icol, cq, cols, ic4 = new("il", 1), new("fl", 1), new("fl", 1), new("fl", 3), new("fl", 1)
-    cpm, cp, cps = sub(cols, 0, 1), sub(cols, 1, 2), sub(cols, 2, 3)
-    ts(icol_i, pcol, 15, A.bitwise_and)
-    vcopy(icol, icol_i)
-    ts(cq, icol_i, -4096.0, A.mult)
-    ts(ic4, icol_i, 4.0, A.mult)
-    mk, mask = new("bl", 256), new("bl", 256)
-    ts(mk, jrow, icol, A.is_gt, 135168.0, A.mult)
-    ts(cols, sub(base, 59, 62), 1024.0, A.mult, cq, A.add)
-    ts(mask, mk, -131072.0, A.add)
+    icol_i, icol, cq, cols, ic4 = new("il", 1), new("fl", 1), new("fl", 1), new("fl", 4), new("fl", 1)
+    cps, cp, cpm = sub(cols, 0, 1), sub(cols, 1, 2), sub(cols, 3, 4)
+    mk, mask = new("hl", 256), new("hl", 256)
     ids = sub(dy, 2, 144, 3)
-    own, c1 = new("fl", 48), new("fl", 48)
-    uo = new("ul", 24)
-    vcopy(uo, uo_i)
-    ts(ids, id_i, ic4, A.add)
-
-    trn = new("fl", 896)
-    tw_o, x0 = new("ul", 56), new("ul", 48)
-    vcopy(tw_o, full("twi", 56))
-    cut = OPT.get("cut", 40)
-    sget(sub(trn, 0, 16 * cut), natinv, sub(tw_o, 0, cut))
-    vget(sub(trn, 16 * cut, 896), natinv, sub(tw_o, cut, 56))
-    ts(x0, full("twi", 48), -1.0, A.add, 1.0 / 3.0, A.mult)
-    ts(own, ids, -8192.0, A.mult, 8192.0 * 1023, A.add)
-    ts(c1, ids, -1.0, A.mult, 1024.0, A.add)
-    ts(("ec", 3, 515, 4), sub(base, 0, 128), pf, A.is_equal)
-
-    dx = [new("fl", 240) for t in range(ROUNDS)]
-    fa, fb, keys = [[new("fl", 48) for t in range(ROUNDS)] for i in range(3)]
+    own, c1 = new("fl", 48), new("hl", 48)
+    uo, tw_o, x0 = new("ul", 24), new("ul", 56), new("ul", 48)
+    trn = new("hl", 896)
+    dx = [new("hl", 240) for t in range(ROUNDS)]
+    fa, fb = [[new("hl", 48) for t in range(ROUNDS)] for i in range(2)]
+    keys = [new("fl", 48) for t in range(ROUNDS)]
     xs = [x0] + [new("ul", 48) for t in range(ROUNDS)]
     toffs = [new("ul", 8) for t in range(ROUNDS + 1)]
 
     def ends(sc, a, b):
         return sub(sc, a + 15, b, 16)
 
+    def group(out, row):
+        scan(out, sub(mask, 0, out[2] - out[1]), row, A.add, A.min)
+
     def lists(t, sc, ssc):
         d = dx[t]
-        n1, mx = new("fl", 48), new("fl", 48)
+        n1, mx, n2, ky = new("fl", 48), new("fl", 48), new("fl", 48), new("fl", 48)
         tw = sub(d, 2, 144, 3)
-        return [lambda: ts(tw, ends(sc, 0, 768), cp, A.subtract),
-                lambda: ts(sub(d, 146, 240, 3), ends(sc, 0, 512), cp, A.subtract),
+        return [lambda: ts(tw, ends(sc, 0, 768), cp, A.add),
+                lambda: ts(sub(d, 146, 240, 3), ends(sc, 0, 512), cp, A.add),
                 lambda: ts(n1, tw, -8192.0, A.mult, 8192.0 * 1023, A.add),
-                lambda: ts(toffs[t], ends(ssc, 0, 128), cp, A.subtract),
+                lambda: ts(toffs[t], ends(ssc, 0, 128), cp, A.add),
                 lambda: tt(mx, n1, own, A.max),
                 lambda: tt(fa[t], sub(d, 98, 240, 3), c1, A.add),
-                lambda: tt(keys[t], mx, tw, A.add),
-                lambda: tt(fb[t], sub(d, 50, 192, 3), tw, A.subtract)]
+                lambda: tt(ky, mx, tw, A.add),
+                lambda: tt(fb[t], sub(d, 50, 192, 3), tw, A.subtract),
+                lambda: ts(n2, tw, -2.0 ** 24, A.mult, 2.0 ** 24 * 1023, A.add),
+                lambda: tt(keys[t], ky, n2, A.min)]
 
     def pick_u(t):
         off = blk(uo, t, 8)
@@ -305,17 +281,61 @@ def rank_program(g, core, T, topo):
             [("qp", c, d)], [("qu", 0, 128), uo])
         run("s", lambda: g.scalar.activation(T.sp[:, c:d], T.su[:, 0:128].indirect(ap(off)), AF.Copy), [("sp", c, d)], [("su", 0, 128), uo])
 
-    sc0, scs = new("fl", 768), new("fl", 128)
-    packs = [(lambda b: lambda: quant(reg("qe", b, 128), reg("se", b, 128), ("ec", 3 - b, 515 - b)))(b) for b in range(4)]
-    scans = [(lambda k: lambda: scan(blk(sc0, k), mask, sub(trn, k, 768, 3)))(k) for k in range(3)]
-    scans.append(lambda: scan(scs, sub(mask, 0, 128), sub(trn, 768, 896)))
-    first = packs + scans + lists(0, sc0, scs)
-    n1, n2 = OPT.get("n1", 4), OPT.get("n2", 6)
-    for c in first[:n1]:
-        c()
-    quant(full("qu", 128), full("su", 128), full("uin", 512))
-    pick_u(0)
-    quant(full("qx", 256), full("sx", 256), full("xin", 1024))
+    sc0, scs = new("hl", 768), new("hl", 128)
+    cut = OPT.get("cut", 40)
+
+    def fills():
+        fill(full("ec", 528), 0.0)
+        fill(sub(pos, 256, 384), 512.0)
+        fill(gz, 0.0)
+        fill(dy, 1024.0)
+        fill(keep, 1.0)
+
+    def codes(q, k):
+        if q == "s":
+            scopy(sub(natinv, k, 768, 3), base, float(k), 4.0)
+        else:
+            ts(sub(natinv, k, 768, 3), base, 4.0, A.mult, float(k), A.add)
+
+    def the_mask():
+        ts(blk(mk, 0, 128), jrow, icol, A.is_lt, 8192.0, A.mult)
+        ts(blk(mk, 1, 128), jrow, icol, A.is_equal, -2048.0, A.mult)
+        for h in range(2):
+            tt(blk(mask, h, 128), blk(mk, 0, 128), blk(mk, 1, 128), A.add)
+
+    def after(row):
+        for k in range(3):
+            scopy(sub(ntn, (k + 2) % 3, 1024, 4), row[k])
+    first = lists(0, sc0, scs)
+    steps = {"fills": fills, "keep": lambda: ts(sub(keep, 0, 48, 3), sub(gz, 0, 16), 0.0, A.mult),
+             "c0": lambda: codes("s", 0), "c1": lambda: codes("s", 1), "c2": lambda: codes("s", 2), "C2": lambda: codes("v", 2),
+             "cs": lambda: scopy(sub(natinv, 768, 896), sub(base, 0, 128), 1025.0, 4.0),
+             "and": lambda: ts(icol_i, pcol, 15, A.bitwise_and), "icol": lambda: vcopy(icol, icol_i),
+             "cq": lambda: ts(cq, icol_i, 15.0, A.is_equal, -2048.0, A.mult), "ic4": lambda: ts(ic4, icol_i, 4.0, A.mult),
+             "cols": lambda: ts(cols, sub(base, 3, 7), 512.0, A.mult, cq, A.add), "mask": the_mask,
+             "uo": lambda: vcopy(uo, uo_i), "ids": lambda: ts(ids, id_i, ic4, A.add),
+             "two": lambda: vcopy(tw_o, full("twi", 56)),
+             "tr": lambda: sget(sub(trn, 0, 16 * cut), natinv, sub(tw_o, 0, cut)),
+             "TR": lambda: vget(sub(trn, 16 * cut, 896), natinv, sub(tw_o, cut, 56)) if cut < 56 else None,
+             "x0": lambda: ts(x0, full("twi", 48), -1.0, A.add, 1.0 / 3.0, A.mult),
+             "own": lambda: ts(own, ids, -8192.0, A.mult, 8192.0 * 1023, A.add), "one": lambda: ts(c1, ids, -1.0, A.mult, 1024.0, A.add),
+             "ec": lambda: ts(("ec", 3, 515, 4), sub(base, 0, 128), pf, A.is_equal),
+             "qu": lambda: quant(full("qu", 128), full("su", 128), full("uin", 512)), "pick": lambda: pick_u(0),
+             "qx": lambda: quant(full("qx", 256), full("sx", 256), full("xin", 1024)),
+             "gs": lambda: group(scs, sub(trn, 768, 896)), "after": lambda: after([sub(trn, k, 768, 3) for k in range(3)]),
+             "h0": lambda: scopy(sub(ntn, 3, 1024, 4), base), "h1": lambda: scopy(sub(f, 3, 1024, 4), base)}
+    for k in range(4):
+        steps["t%d" % k] = (lambda k: lambda: scopy(sub(tab, 1024 + k, 2048, 4), base, float((k + 2) % 3), 4.0))(k)
+        steps["e%d" % k] = (lambda b: lambda: quant(reg("qe", b, 128), reg("se", b, 128), ("ec", 3 - b, 515 - b)))(k)
+        steps["g%d" % k] = (lambda k: lambda: group(blk(sc0, k), sub(trn, k, 768, 3)))(k)
+    for k in range(10):
+        steps["l%d" % k] = first[k]
+    start = steps
+
+    def do(names):
+        for name in names.split():
+            start[name]()
+    do(OPT.get("o1", "fills keep cs c0 C2 and c1 t0 uo cq t1 icol ic4 two x0 cols tr TR ids ec qu mask pick one qx g1 after"))
     dma("y", T.qw[:, :].bitcast(dt.uint8), T.wc[:, :], [full("qw", 512)], [], "ld3")
     dma("y", T.sw[:, :], T.ws[:, :], [full("sw", 512)], [], "ld4")
 
@@ -353,6 +373,12 @@ def rank_program(g, core, T, topo):
     def score(t):
         mm(4, reg("qp", t, 128), reg("sp", t, 128), reg("qx", t, 256), reg("sx", t, 256), 256)
 
+    def signs(q, out, scores):
+        if q == "v":
+            ts(out, scores, 0.0, A.is_gt, 1024.0, A.mult)
+        else:
+            run("s", lambda: g.scalar.activation(ap(out), ap(scores), AF.Sign, bias=-(2.0 ** -110)), [out], [scores])
+
     def zreg(t, b, a, e):
         return ("z", (4 * t + b) * ZW + a, (4 * t + b) * ZW + e)
 
@@ -360,185 +386,211 @@ def rank_program(g, core, T, topo):
     send_state(0)
     iota(sub(tab, 0, 1024), [[1, 1024]], 0, 0, True)
     iota(sub(f, 1024, 1536), [[1, 512]], 1024, 0, True)
-    for k in range(3):
-        scopy(sub(ntn, (k + 2) % 3, 1024, 4), sub(trn, k, 768, 3))
-
     nsc = sc0
-    for c in first[n1:n2]:
-        c()
+    do(OPT.get("o2", "g2 g0"))
 
     for t in range(ROUNDS):
         last = t == ROUNDS - 1
-        po = new("bl", 768)
-        ts(sub(pos, 0, 256), ("ps", 2048, 2304), 0.0, A.is_gt, 2048.0, A.mult)
+        po, spos, so = new("hl", 768), new("hl", 256), new("hl", 768)
         if t == 0:
+            signs(OPT.get("p0", "v"), sub(pos, 0, 256), ("ps", 2048, 2304))
             part = [sub(po, k, 768, 3) for k in range(3)]
             sget(po, pos, xs[0])
-            for c in first[n2:]:
-                c()
+            group(spos, sub(pos, 0, 256))
+            do(OPT.get("o3", "l0 l1 gs e3 h1 t3 own h0 l2 l3 e1 e2 l4 e0 l8 l6 l7 l5 l9 t2"))
         else:
             part = [blk(po, k) for k in range(3)]
+            group(spos, sub(pos, 0, 256))
             for k in range(3):
                 get["ssv"[k]](part[k], pos, blk(xs[t], k, 16))
         for b in range(4):
             mm(b, reg("qe", b, 128), reg("se", b, 128), reg("qx", t, 256), reg("sx", t, 256), 256)
-        spos, so = new("bl", 256), new("bl", 768)
-        scan(spos, mask, sub(pos, 0, 256))
-        sv, so_g, svm = new("fl", 16), new("fl", 48), new("fl", 48)
-        ts(sv, ends(spos, 0, 256), cps, A.subtract, -1.0 / 1024, A.mult)
-        if t:
-            scan(blk(so, 0), mask, part[0])
-        for k in range(3):
-            tt(blk(svm, k, 16), blk(keys[t], k, 16), sv, A.mult)
-        for k in ((2, 1) if t else (0, 1, 2)):
-            scan(blk(so, k), mask, part[k])
-        ts(so_g, ends(so, 0, 768), cps, A.subtract, 1.0 / 1024, A.mult)
-        if t == 0:
-            scopy(sub(ntn, 3, 1024, 4), base)
-            scopy(sub(f, 3, 1024, 4), base)
-            before(th, 4)
         for b in range(4):
             scopy(zreg(t, b, 0, 256), ("ps", 512 * b, 512 * b + 256))
-        pk = new("fl", 48)
-        tt(pk, so_g, svm, A.mult)
-        ra, rb, r = new("fl", 16), new("fl", 16), new("il", 16)
-        tt(ra, blk(pk, 0, 16), blk(pk, 1, 16), A.max)
-        ts(rb, blk(pk, 2, 16), 1.0, A.max)
-        tt(r, ra, rb, A.max)
-        m_o, c_i, oc, cn, rd = new("ul", 16), new("il", 16), new("ul", 16), new("ul", 16), new("fl", 16)
+        wants, pk, rk = new("fl", 48), new("fl", 48), new("fl", 48)
+        sign = {"s": lambda k: group(blk(so, k), part[k]),
+                "w": lambda k: tt(blk(wants, k, 16), ends(so, 256 * k, 256 * k + 256), ends(spos, 0, 256), A.not_equal),
+                "p": lambda k: tt(sub(pk, k, 48, 3), blk(wants, k, 16), blk(keys[t], k, 16), A.mult)}
+        for step in (OPT.get("sorder", "s0 s2 w0 w2 s1 p0 w1 p2 p1") if t else "s0 s1 s2 w0 w1 w2 p0 p1 p2").split():
+            sign[step[0]](int(step[1]))
+        scan(rk, keep, pk, A.mult, A.max)
+        r = sub(rk, 2, 48, 3)
+        m_o, r_i, c_i, oc, cn, rd = new("ul", 16), new("il", 16), new("il", 16), new("ul", 16), new("ul", 16), new("fl", 16)
         ts(m_o, r, 1.0 / 8192, A.mult)
-        ts(c_i, r, 2047, A.bitwise_and)
-        rr, ro, rs, tq, tqs = [new("fl", 256) for i in range(5)]
+        vcopy(r_i, r)
+        rr = new("fl", 256)
+        ro, rs, tq, tqs = [new("hl", 256) for i in range(4)]
+        fz = OPT.get("fz", 0)
         sget(rr, sub(tab, 0, 1024), m_o)
         icx = [sub(gz, 48 * i + 1, 48 * i + 48, 3) for i in range(4)]
-        tt(icx[0], blk(pk, 1, 16), r, A.is_equal)
+        tt(icx[0], blk(keys[t], 1, 16), r, A.is_equal)
+        tt(icx[1], blk(keys[t], 2, 16), r, A.is_equal)
+        ts(c_i, r_i, 2047, A.bitwise_and)
+        tt(icx[2], blk(keys[t], 0, 16), r, A.is_equal)
+        tt(icx[3], blk(keys[t], 1, 16), r, A.is_equal)
         ts(oc, c_i, QUARTER, A.mult)
         vcopy(cn, c_i)
-        sget(ro, rr, oc)
-        sget(tq, ntn, cn)
-        for i, k in ((1, 2), (2, 0), (3, 1)):
-            tt(icx[i], blk(pk, k, 16), r, A.is_equal)
-        ts(rd, m_o, cp, A.add)
+        if not fz:
+            sget(ro, rr, oc)
+        tqv = OPT.get("tqv", 0)
+        if not tqv:
+            sget(tq, ntn, cn)
         ia = sub(gz, 49, 192, 3)
+        if fz == 1:
+            run("v", lambda: g.vector.tensor_tensor(ap(ro), ap(rr).indirect(ap(oc)), ap(rr), A.is_equal), [ro], [rr, oc])
+        if not fz:
+            ts(rd, m_o, cp, A.subtract)
         tt(sub(dy, 1, 144, 3), fa[t], ia, A.mult)
         tt(sub(dx[t], 1, 144, 3), fb[t], ia, A.mult)
+        if fz == 2:
+            run("v", lambda: g.vector.tensor_tensor(ap(ro), ap(rr).indirect(ap(oc)), ap(rr), A.is_equal), [ro], [rr, oc])
+        if tqv:
+            vget(tq, ntn, cn)
         for b in range(4):
             mm(4 + b, reg("qe", b, 128), reg("se", b, 128), reg("lq", t, 512), reg("lsc", t, 512), 512)
-        todo = [0, 1, 2, 3]
-
-        def unpack(q, cnt):
-            for i in range(cnt):
-                b = todo.pop(0)
-                copy[q](reg("nz", 4 * t + b, 512), reg("ps", 4 + b, 512))
-        unpack("s", OPT.get("nz1", 0) if t else 0)
-        ys, yo, xx, xo = new("fl", 144), new("ul", 48), new("fl", 144), new("ul", 48)
-        scan(rs, mask, ro)
-        for k in range(3):
-            tt(sub(gz, 48 * k + 2, 48 * k + 48, 3), ends(rs, 0, 256), rd, A.is_equal)
-        scan(ys, sub(gz, 0, 144), dy, A.mult, A.add)
-        vcopy(yo, sub(ys, 2, 144, 3))
-        nf = OPT.get("nf", 40)
+        ys, yo, xx, xo = new("hl", 144), new("ul", 48), new("hl", 144), new("ul", 48)
+        nts, ssc, sd = new("hl", 128), new("hl", 128), new("snd", 8)
+        old, nth, nsc = nsc, new("hl", 768), new("hl", 768)
+        x = xs[t + 1]
+        nf = OPT.get("nf", 32)
+        nn = OPT.get("nn", 28)
 
         def expand(q, a, b):
             while a < b:
                 k, e = a // 16, min(b, a // 16 * 16 + 16)
                 get[q](sub(f, k + 64 * (a - 16 * k), 64 * (e - 16 * k), 4), tab, sub(yo, a, e))
                 a = e
-        expand("s", 0, nf)
-        scan(tqs, mask, tq)
-        for k in range(3):
-            tt(sub(dx[t], 48 * k, 48 * k + 48, 3), ends(tqs, 0, 256), ends(nsc, 256 * k, 256 * k + 256), A.subtract)
-        scan(xx, sub(gz, 0, 144), sub(dx[t], 0, 144), A.mult, A.add)
-        vcopy(xo, sub(xx, 2, 144, 3))
-        expand("v", nf, 48)
-        nts, ssc, sd = new("fl", 128), new("fl", 128), new("snd", 8)
-        vget(nts, f, toffs[t])
-        nn = OPT.get("nn", 2)
-        for k in range(nn):
-            sget(sub(ntn, (k + 2) % 3, 1024, 4), f, blk(xo, k, 16))
-        scan(ssc, sub(mask, 0, 128), nts)
-        ts(sub(sd, 0, 4), ends(ssc, 0, 64), cpm, A.subtract, QUARTER, A.mult)
-        ts(sub(sd, 4, 8), ends(ssc, 64, 128), cp, A.subtract, QUARTER, A.mult)
-        send((ap(reg("lnd", 2 * t + 1, 4)), ap(sub(sd, 0, 4))), (ap(reg("lnd", 2 * t, 4)), ap(sub(sd, 4, 8))), [sd], "al%d" % t)
-        if t == 0:
-            iota(sub(nattab, 0, 1024), [[3, 256], [1, 4]], 0, 0, True)
-        if t == 1:
-            iota(sub(nattab, 1024, 1536), [[1, 128], [0, 4]], 768, 0, True)
-        for k in range(nn, 3):
-            vget(sub(ntn, (k + 2) % 3, 1024, 4), f, blk(xo, k, 16))
-        nsc = new("fl", 768)
-        for k in range(3):
-            scan(blk(nsc, k), mask, sub(ntn, (k + 2) % 3, 1024, 4))
-        x = xs[t + 1]
-        ts(x, ends(nsc, 0, 768), cp, A.subtract, QUARTER, A.mult)
-        if t == 0:
-            dma("y", T.vin[:, :], T.v[:, :], [full("vin", 512)], [nsc], "ld5")
+
+        def flags():
             for k in range(3):
-                ts(("m3", k, 768, 3), jrow, 0.0, A.mult, 0.0 if k else -1.0e29, A.add)
-        nv = OPT.get("nzv", 0)
-        unpack("s", len(todo) - nv)
-        g1 = OPT.get("gap1", 4)
+                if fz:
+                    ts(sub(gz, 48 * k + 2, 48 * k + 48, 3), ends(rs, 0, 256), cp, A.add)
+                else:
+                    tt(sub(gz, 48 * k + 2, 48 * k + 48, 3), ends(rs, 0, 256), rd, A.is_equal)
+
+        def changes():
+            for k in range(3):
+                tt(sub(dx[t], 48 * k, 48 * k + 48, 3), ends(tqs, 0, 256), ends(old, 256 * k, 256 * k + 256), A.subtract)
+
+        def post():
+            ts(sub(sd, 0, 4), ends(ssc, 0, 64), cpm, A.add, QUARTER, A.mult)
+            ts(sub(sd, 4, 8), ends(ssc, 64, 128), cp, A.add, QUARTER, A.mult)
+            send((ap(reg("lnd", 2 * t + 1, 4)), ap(sub(sd, 0, 4))), (ap(reg("lnd", 2 * t, 4)), ap(sub(sd, 4, 8))), [sd], "al%d" % t)
+        steps = {"rs": lambda: group(rs, ro), "go": flags,
+                 "ys": lambda: scan(ys, sub(gz, 0, 144), dy, A.mult, A.add), "yo": lambda: vcopy(yo, sub(ys, 2, 144, 3)),
+                 "f": lambda: expand("s", 0, nf), "F": lambda: expand("v", nf, 48),
+                 "tq": lambda: group(tqs, tq), "ux": changes,
+                 "xx": lambda: scan(xx, sub(gz, 0, 144), sub(dx[t], 0, 144), A.mult, A.add), "xo": lambda: vcopy(xo, sub(xx, 2, 144, 3)),
+                 "SL": lambda: vget(nts, f, toffs[t]), "sl": lambda: sget(nts, f, toffs[t]),
+                 "ss": lambda: group(ssc, nts), "post": post,
+                 "n": lambda: sget(sub(nth, 0, 16 * nn), f, sub(xo, 0, nn)), "N": lambda: vget(sub(nth, 16 * nn, 768), f, sub(xo, nn, 48)),
+                 "x": lambda: ts(x, ends(nsc, 0, 768), cp, A.add, QUARTER, A.mult)}
+        for k in range(3):
+            steps["n%d" % k] = (lambda k: lambda: sget(blk(nth, k), f, blk(xo, k, 16)))(k)
+            steps["N%d" % k] = (lambda k: lambda: vget(blk(nth, k), f, blk(xo, k, 16)))(k)
+            steps["s%d" % k] = (lambda k: lambda: group(blk(nsc, k), blk(nth, k)))(k)
+        nothing = lambda: None
         if last:
             cl, s_o, otb = new("ul", 48), new("ul", 8), new("fl", 896)
-            later = [lambda: ts(cl, ends(nsc, 0, 768), cp, A.subtract), lambda: ts(s_o, ends(ssc, 0, 128), cp, A.subtract),
-                     lambda: quant(full("qv", 128), full("svp", 128), full("vin", 512)),
-                     lambda: vget(sub(otb, 0, 768, 3), nattab, blk(cl, 0, 16)),
-                     lambda: vget(sub(otb, 1, 768, 3), nattab, blk(cl, 1, 16))]
-            g1 = OPT.get("gapl", 4)
+            later = [lambda: ts(cl, ends(nsc, 0, 768), cp, A.add), lambda: quant(full("qv", 128), full("svp", 128), full("vin", 512)),
+                     nothing, lambda: ts(s_o, ends(ssc, 0, 128), cp, A.add),
+                     lambda: vget(sub(otb, 0, 768, 3), nattab, blk(cl, 0, 16)), nothing,
+                     nothing, nothing, nothing, lambda: vget(sub(otb, 1, 768, 3), nattab, blk(cl, 1, 16))]
         else:
             later = lists(t + 1, nsc, ssc)
-        for c in later[:g1]:
-            c()
-        unpack("v", nv)
         tb = 1024 * t
         win = [zreg(t, b, 0, ZW) for b in range(4)]
         outs = [("mt", tb + b, tb + 1024, 4) for b in range(4)]
         ma, mb = [reg("ma", 4 * t + b, 256) for b in range(4)], [reg("mb", 4 * t + b, 256) for b in range(4)]
         mg, ms = [reg("mg", 2 * t + b % 2, 768) for b in range(4)], [reg("ms", 2 * t + b % 2, 768) for b in range(4)]
 
-        def side_by_side(b):
-            for k in range(3):
-                sget(sub(mg[b], k, 768, 3), win[b], blk(x, k, 16))
-        steps = {"B": lambda b: vget(zreg(t, b, 256, 384), reg("nz", 4 * t + b, 512), reg("lnd", t, 8)),
-                 "b": lambda b: sget(zreg(t, b, 256, 384), reg("nz", 4 * t + b, 512), reg("lnd", t, 8)),
-                 "G": lambda b: vget(ma[b], win[b], blk(x, 0, 16)),
-                 "g": lambda b: sget(ma[b], win[b], blk(x, 0, 16)),
-                 "M": lambda b: vmax(mb[b], win[b], blk(x, 1, 16), ma[b]),
-                 "O": lambda b: vmax(outs[b], win[b], blk(x, 2, 16), mb[b]),
-                 "s": side_by_side,
-                 "R": lambda b: scan(ms[b], full("m3", 768), mg[b]),
-                 "C": lambda b: vcopy(outs[b], sub(ms[b], 2, 768, 3))}
-        for step in OPT.get("morder", "b2 B0 g2 B1 b3 G0 g1 M2 M0 s3 O2 M1 O0 R3 O1 C3").split():
-            steps[step[0]](int(step[1]))
-        quant(reg("qm", t, 256), reg("sm", t, 256), reg("mt", t, 1024))
-        for b in range(4):
-            mm(4 + b, reg("qw", b, 128), reg("sw", b, 128), reg("qm", t, 256), reg("sm", t, 256), 256)
-        for c in later[g1:]:
-            c()
-        if t == 0:
-            pick_u(1)
-            pick_u(2)
-        if last:
-            sget(sub(otb, 2, 768, 3), nattab, blk(cl, 2, 16))
-            sget(sub(otb, 768, 896), nattab, s_o)
-            dma("y", T.ot[:, :], T.fl[0:128:16, otb[1]:otb[2]], [], [otb], "out")
-        for b in range(4):
-            tmp = reg("tm", b, 256)
-            wb = ("ps", 2048 + 512 * b, 2304 + 512 * b)
-            run("s", lambda: g.scalar.activation(ap(tmp), ap(wb), AF.Relu, scale=0.015625), [tmp], [wb])
-            tt(("xt", tb + b, tb + 1024, 4), tmp, ("ps", 512 * b, 512 * b + 256), A.add)
-        quant(reg("qx", t + 1, 256), reg("sx", t + 1, 256), reg("xt", t, 1024))
-        if not last:
-            score(t + 1)
-            send_state(t + 1)
+        def once():
+            if t == 0:
+                dma("y", T.vin[:, :], T.v[:, :], [full("vin", 512)], [x], "ld5")
+                for k in range(3):
+                    ts(("m3", k, 768, 3), mask, 0.0, A.mult, 0.0 if k else -1.0e29, A.add)
+
+        def numbers():
+            if last:
+                sget(sub(otb, 2, 768, 3), nattab, blk(cl, 2, 16))
+                sget(sub(otb, 768, 896), nattab, s_o)
+
+        def half(h):
+            c0 = tb + 4 * HW * h
+            w = HW // 16
+            steps["O1" + "ab"[h]] = lambda: vmax(("mt", c0 + 1, c0 + 4 * HW, 4), win[1], sub(x, 32 + w * h, 32 + w * h + w), blk(mb[1], h, HW))
+            steps["C3" + "ab"[h]] = lambda: vcopy(("mt", c0 + 3, c0 + 4 * HW, 4), sub(ms[3], 3 * HW * h + 2, 3 * HW * (h + 1), 3))
+            steps["p" + "ab"[h]] = lambda: quant(reg("qm", H * t + h, HW), reg("sm", H * t + h, HW), reg("mt", H * t + h, 4 * HW))
+        for h in range(H):
+            half(h)
+        by_b = {"U": lambda b: vcopy(reg("nz", 4 * t + b, 512), reg("ps", 4 + b, 512)),
+                "u": lambda b: scopy(reg("nz", 4 * t + b, 512), reg("ps", 4 + b, 512)),
+                "B": lambda b: vget(zreg(t, b, 256, 384), reg("nz", 4 * t + b, 512), reg("lnd", t, 8)),
+                "b": lambda b: sget(zreg(t, b, 256, 384), reg("nz", 4 * t + b, 512), reg("lnd", t, 8)),
+                "G": lambda b: vget(ma[b], win[b], blk(x, 0, 16)),
+                "g": lambda b: sget(ma[b], win[b], blk(x, 0, 16)),
+                "M": lambda b: vmax(mb[b], win[b], blk(x, 1, 16), ma[b]),
+                "O": lambda b: vmax(outs[b], win[b], blk(x, 2, 16), mb[b]),
+                "i": lambda b: sget(sub(mg[b], 0, 768, 3), win[b], blk(x, 0, 16)),
+                "j": lambda b: sget(sub(mg[b], 1, 768, 3), win[b], blk(x, 1, 16)),
+                "k": lambda b: sget(sub(mg[b], 2, 768, 3), win[b], blk(x, 2, 16)),
+                "R": lambda b: scan(ms[b], full("m3", 768), mg[b]),
+                "C": lambda b: vcopy(outs[b], sub(ms[b], 2, 768, 3))}
+        for name in by_b:
+            for b in range(4):
+                steps[name + str(b)] = (lambda fn, b: lambda: fn(b))(by_b[name], b)
+        for k in range(10):
+            steps["l%d" % k] = later[k]
+        steps.update({"once": once, "ot": numbers, "pick": nothing if last else lambda: pick_u(t + 1)})
+        def layer(h):
+            for b in range(4):
+                mm(4 + b, reg("qw", b, 128), reg("sw", b, 128), reg("qm", H * t + h, HW), reg("sm", H * t + h, HW), HW)
+            for b in range(4):
+                tmp, wb = reg("tm", H * b + h, HW), ("ps", 2048 + 512 * b, 2048 + 512 * b + HW)
+                run("s", lambda: g.scalar.activation(ap(tmp), ap(wb), AF.Relu, scale=0.015625), [tmp], [wb])
+
+        def state(h):
+            c0 = tb + 4 * HW * h
+            for b in range(4):
+                tt(("xt", c0 + b, c0 + 4 * HW, 4), reg("tm", H * b + h, HW), ("ps", 512 * b + HW * h, 512 * b + HW * h + HW), A.add)
+
+        def pack(h):
+            q = reg("qx", H * (t + 1) + h, HW)
+            quant(q, reg("sx", H * (t + 1) + h, HW), reg("xt", H * t + h, 4 * HW))
+            if last:
+                dma("y", T.oc[:, 4 * HW * h:4 * HW * (h + 1)], u8(q), [], [q], "out")
+            if h == H - 1 and not last:
+                send_state(t + 1)
+
+        def scores(h, q):
+            w, ws = (full("qv", 128), full("svp", 128)) if last else (reg("qp", t + 1, 128), reg("sp", t + 1, 128))
+            mm(4 + h, w, ws, reg("qx", H * (t + 1) + h, HW), reg("sx", H * (t + 1) + h, HW), HW)
+            got = ("ps", 2048 + 512 * h, 2048 + 512 * h + HW)
+            if last:
+                copy["sv"[h]](reg("yo", h, HW), got)
+                dma("sy"[h], T.y[:, HW * h:HW * h + HW], ap(reg("yo", h, HW)), [], [reg("yo", h, HW)], "out")
+            else:
+                signs(q, blk(pos, h, HW), got)
+
+        def tables():
+            if t == 0:
+                iota(sub(nattab, 0, 1024), [[3, 256], [1, 4]], 0, 0, True)
+            if t == 1:
+                iota(sub(nattab, 1024, 1536), [[1, 128], [0, 4]], 768, 0, True)
+            if last:
+                dma("y", T.ot[:, :], T.fl[0:128:16, otb[1]:otb[2]], [], [otb], "out")
+        for h in range(H):
+            for name, fn in (("r", layer), ("A", state), ("Q", pack), ("z", lambda h: scores(h, "s")), ("Z", lambda h: scores(h, "v"))):
+                steps[name + "ab"[h]] = (lambda fn, h: lambda: fn(h))(fn, h)
+        for k in range(3):
+            steps["a%d" % k] = nothing if last else (lambda k: lambda: scopy(sub(ntn, (k + 2) % 3, 1024, 4), blk(nth, k)))(k)
+        steps["tab"] = tables
+        for step in OPT.get("forder", "rs go ys tq yo f ux F xx xo SL n ss post N s0 s2 s1 x u0 u1 u2 u3 l0 once l2 l3 l1 l4 l8 l6 l5 l7 l9 b2 g2 b3 B0 B1 G0 M2 g1 i3 j3 k3 M0 O2 M1 O0 R3 ot O1a C3a C3b pa O1b pick pb tab ra Aa rb a0 a1 a2 Qa Ab Qb Za Zb").split():
+            steps[step]()
 
     q, s = reg("qx", ROUNDS, 256), reg("sx", ROUNDS, 256)
-    mm(0, full("qv", 128), full("svp", 128), q, s, 256)
-    dma("y", T.oc[:, :], u8(q), [], [q], "out")
     for k in range(4):
         dma("y" if k % 2 else "s", T.osc[4 * k:4 * k + 4, :], T.sx[32 * k:32 * k + 4, s[1]:s[2]], [], [s], "out")
-    vcopy(full("yo", 256), ("ps", 0, 256))
-    dma("y", T.y[:, :], T.yo[:, :], [], [full("yo", 256)], "out")
     for s in sorted(total):
         if known["g"].get(s, 0) < total[s]:
             g.wait_ge(T.sem[s], total[s])

from concourse.bass import DstId, RemoteDMATransfer
from concourse.mybir import dt, AluOpType, ActivationFunctionType

ROUNDS = 3
ZW = 384
QUARTER = 0.2499
OPT = {}
H = OPT.get("H", 2)
HW = 256 // H

SCRATCH = {
    "xin": ("sbuf", [128, 1024], "bfloat16"),
    "uin": ("sbuf", [128, 512], "bfloat16"),
    "vin": ("sbuf", [128, 512], "bfloat16"),
    "xt": ("sbuf", [128, 3072], "bfloat16"),
    "mt": ("sbuf", [128, 3072], "bfloat16"),
    "z": ("sbuf", [128, 12 * ZW], "bfloat16"),
    "nz": ("sbuf", [128, 12 * 512], "bfloat16"),
    "ma": ("sbuf", [128, 12 * 256], "bfloat16"),
    "mb": ("sbuf", [128, 12 * 256], "bfloat16"),
    "mg": ("sbuf", [128, 6 * 768], "bfloat16"),
    "ms": ("sbuf", [128, 6 * 768], "bfloat16"),
    "m3": ("sbuf", [128, 768], "bfloat16"),
    "tm": ("sbuf", [128, 1024], "float32"),
    "yo": ("sbuf", [128, 256], "float32"),
    "cb": ("sbuf", [128, 400], "float32"),
    "ec": ("sbuf", [128, 528], "bfloat16"),
    "qe": ("sbuf", [128, 512], "float8_e4m3fn_x4"), "se": ("sbuf", [128, 512], "uint8"),
    "qu": ("sbuf", [128, 128], "float8_e4m3fn_x4"), "su": ("sbuf", [128, 128], "uint8"),
    "qp": ("sbuf", [128, 384], "float8_e4m3fn_x4"), "sp": ("sbuf", [128, 384], "uint8"),
    "qv": ("sbuf", [128, 128], "float8_e4m3fn_x4"), "svp": ("sbuf", [128, 128], "uint8"),
    "qw": ("sbuf", [128, 512], "float8_e4m3fn_x4"), "sw": ("sbuf", [128, 512], "uint8"),
    "qx": ("sbuf", [128, 1024], "float8_e4m3fn_x4"), "sx": ("sbuf", [128, 1024], "uint8"),
    "qm": ("sbuf", [128, 768], "float8_e4m3fn_x4"), "sm": ("sbuf", [128, 768], "uint8"),
    "lq": ("sbuf", [128, 1536], "float8_e4m3fn_x4"), "lsc": ("sbuf", [128, 1536], "uint8"),
    "twi": ("sbuf", [128, 56], "int32"),
    "fl": ("sbuf", [128, 11000], "float32"),
    "il": ("sbuf", [128, 600], "int32"),
    "bl": ("sbuf", [128, 384], "bfloat16"),
    "ul": ("sbuf", [128, 1800], "uint16"),
    "hl": ("sbuf", [128, 20000], "float16"),
    "snd": ("sbuf", [128, 48], "uint16"),
    "lnd": ("sbuf", [128, 24], "uint16"),
    "ps": ("psum", [128, 4096], "float32"),
}
SEMAPHORES = (["sv", "ss", "st", "sg", "loc", "out"] + ["ld%d" % i for i in range(6)]
              + ["aq%d" % t for t in range(3)] + ["al%d" % t for t in range(3)])


def rank_program(g, core, T, topo):
    rank = T.rank_of(core)
    if rank is None:
        return
    A = AluOpType
    AF = ActivationFunctionType
    cores = T.cores
    n = len(cores)
    up, down = cores[(rank + 1) % n], cores[(rank + n - 1) % n]

    queues = {"v": g.vector, "s": g.scalar, "t": g.tensor, "g": g, "y": g.sync}
    qsem = {"v": "sv", "s": "ss", "t": "st", "g": "sg"}
    total = {}
    known = {q: {} for q in queues}
    touched = {}

    def span(r):
        if r[0] == "ps":
            return r[1] // 512 * 512, (r[2] + 511) // 512 * 512, 1
        return r[1], r[2], (r[3] if len(r) > 3 else 1)

    def needs(q, dma, ins, outs):
        found = []
        for writing, regs in ((False, ins), (True, outs)):
            for r in regs:
                a, b, st = span(r)
                for (c, d, st2, w, oq, odma, op) in touched.get(r[0], ()):
                    if c >= b or d <= a:
                        continue
                    if st == st2 and st > 1 and (a - c) % st and not dma and not odma:
                        continue
                    if r[0] == "ps":
                        if oq == q and (writing or not w):
                            continue
                    elif not writing and not w:
                        continue
                    found.append(op)
        return found

    def wait_for(q, ops):
        want = {}
        for op in ops:
            s = op["sem"]
            if known[q].get(s, 0) >= op["cnt"]:
                continue
            cnt = op["cnt"] if s in ("sv", "ss", "st", "sg") else max(op["cnt"], total.get(s, 0))
            if s not in want or want[s][0] < cnt:
                want[s] = (cnt, op["clk"])
        for s in list(want):
            if any(s2 != s and want[s2][1].get(s, 0) >= want[s][0] for s2 in want):
                del want[s]
        for s in sorted(want):
            queues[q].wait_ge(T.sem[s], want[s][0])
        for op in ops:
            for k, c in op["clk"].items():
                if known[q].get(k, 0) < c:
                    known[q][k] = c
        for s in want:
            if known[q].get(s, 0) < want[s][0]:
                known[q][s] = want[s][0]

    def note(q, dma, ins, outs, op):
        for w, regs in ((False, ins), (True, outs)):
            for r in regs:
                a, b, st = span(r)
                touched.setdefault(r[0], []).append((a, b, st, w, q, dma, op))

    def run(q, fn, outs, ins):
        wait_for(q, needs(q, False, ins, outs))
        s = qsem[q]
        total[s] = total.get(s, 0) + 1
        fn().then_inc(T.sem[s], 1)
        clk = dict(known[q])
        clk[s] = total[s]
        note(q, False, ins, outs, {"sem": s, "cnt": total[s], "clk": clk})

    def dma(q, out_ap, in_ap, outs, ins, sem):
        wait_for(q, needs(q, True, ins, outs))
        total[sem] = total.get(sem, 0) + 16
        queues[q].dma_start(out_ap, in_ap).then_inc(T.sem[sem], 16)
        note(q, True, ins, outs, {"sem": sem, "cnt": total[sem], "clk": dict(known[q])})

    def arrive(sem, cnt, outs):
        total[sem] = total.get(sem, 0) + cnt
        note("net", True, [], outs, {"sem": sem, "cnt": total[sem], "clk": {}})

    def ap(r):
        if len(r) > 3 and r[3] != 1:
            return T[r[0]][:, r[1]:r[2]:r[3]]
        return T[r[0]][:, r[1]:r[2]]

    def u8(r):
        return ap(r).bitcast(dt.uint8)

    unit = {"fl": 16, "il": 16, "bl": 32, "hl": 32, "ul": 32, "snd": 16}
    free = {b: 0 for b in unit}

    def new(buf, w):
        a = free[buf]
        free[buf] = a + (w + unit[buf] - 1) // unit[buf] * unit[buf]
        if free[buf] > SCRATCH[buf][1][1]:
            raise ValueError(buf)
        return (buf, a, a + w)

    def sub(r, a, b, s=1):
        return (r[0], r[1] + a, r[1] + b, s)

    def blk(r, k, w=256):
        return sub(r, w * k, w * k + w)

    def reg(name, k, w):
        return (name, w * k, w * k + w)

    def num(x, ins):
        if isinstance(x, tuple):
            ins.append(x)
            return ap(x)
        return x

    def ts(out, in0, s1, op0, s2=None, op1=None):
        ins = [in0]
        a1 = num(s1, ins)
        a2 = num(s2, ins)
        if op1 is None:
            run("v", lambda: g.vector.tensor_scalar(ap(out), ap(in0), a1, None, op0), [out], ins)
        else:
            run("v", lambda: g.vector.tensor_scalar(ap(out), ap(in0), a1, a2, op0, op1), [out], ins)

    def tt(out, in0, in1, op):
        run("v", lambda: g.vector.tensor_tensor(ap(out), ap(in0), ap(in1), op), [out], [in0, in1])

    def vcopy(out, in0):
        run("v", lambda: g.vector.tensor_copy(ap(out), ap(in0)), [out], [in0])

    def fill(out, x):
        run("v", lambda: g.vector.memset(ap(out), x), [out], [])

    def scan(out, d0, d1, op0=A.add, op1=A.max):
        run("v", lambda: g.vector.tensor_tensor_scan(ap(out), ap(d0), ap(d1), 0.0, op0, op1), [out], [d0, d1])

    def scopy(out, in0, bias=None, scale=1.0):
        if bias is None:
            run("s", lambda: g.scalar.activation(ap(out), ap(in0), AF.Copy), [out], [in0])
        else:
            run("s", lambda: g.scalar.activation(ap(out), ap(in0), AF.Identity, bias=bias, scale=scale), [out], [in0])

    def vget(out, win, off):
        run("v", lambda: g.vector.tensor_copy(ap(out), ap(win).indirect(ap(off))), [out], [win, off])

    def sget(out, win, off):
        run("s", lambda: g.scalar.activation(ap(out), ap(win).indirect(ap(off)), AF.Copy), [out], [win, off])

    def vmax(out, win, off, in1):
        run("v", lambda: g.vector.tensor_tensor(ap(out), ap(win).indirect(ap(off)), ap(in1), A.max), [out], [win, off, in1])

    def iota(out, pattern, base, cm, flag=False):
        if flag:
            run("g", lambda: g.iota(ap(out), pattern, base, cm, allow_small_or_imprecise_dtypes=True), [out], [])
        else:
            run("g", lambda: g.iota(ap(out), pattern, base, cm), [out], [])

    def quant(codes, scales, tile):
        run("v", lambda: g.vector.quantize_mx(ap(codes), ap(scales), ap(tile)), [codes, scales], [tile])

    def mm(bank, w, ws, x, xs, width):
        out = ("ps", 512 * bank, 512 * bank + width)
        run("t", lambda: g.tensor.matmul_mx(ap(out), ap(w), ap(ws), ap(x), ap(xs), True, True), [out], [w, ws, x, xs])

    get = {"v": vget, "s": sget}
    copy = {"v": vcopy, "s": scopy}

    full = lambda name, w: (name, 0, w)
    dma("y", T.twi[:, :], T.tw[:, :], [full("twi", 56)], [], "ld0")
    dma("s", T.uin[:, :], T.u[:, :], [full("uin", 512)], [], "ld2")
    dma("y", T.xin[:, :], T.x[:, :], [full("xin", 1024)], [], "ld1")

    base, pf = ("cb", 0, 256), ("cb", 256, 257)
    pcol, uo_i, id_i = new("il", 1), new("il", 24), new("il", 48)
    jrow = new("hl", 128)
    iota(base, [[1, 256]], 0, 0, True)
    iota(pcol, [[0, 1]], 0, 1)
    iota(uo_i, [[1, 3], [16, 8]], 0, 0)
    iota(("cb", 272, 400), [[0, 8], [1, 16]], -1, 0, True)
    iota(id_i, [[1, 3], [64, 16]], 0, 0)
    iota(pf, [[0, 1]], 0, 1, True)
    jrow = ("cb", 272, 400)

    pos = new("bl", 384)
    gz = new("hl", 192)
    dy = new("hl", 144)
    keep = new("fl", 48)
    natinv = new("fl", 896)
    tab, f, ntn, nattab = new("fl", 2048), new("fl", 1536), new("fl", 1024), new("fl", 1536)
    icol_i, icol, cq, cols, ic4 = new("il", 1), new("fl", 1), new("fl", 1), new("fl", 4), new("fl", 1)
    cps, cp, cpm = sub(cols, 0, 1), sub(cols, 1, 2), sub(cols, 3, 4)
    mk, mask = new("hl", 256), new("hl", 256)
    ids = sub(dy, 2, 144, 3)
    own, c1 = new("fl", 48), new("hl", 48)
    uo, tw_o, x0 = new("ul", 24), new("ul", 56), new("ul", 48)
    trn = new("hl", 896)
    dx = [new("hl", 240) for t in range(ROUNDS)]
    fa, fb = [[new("hl", 48) for t in range(ROUNDS)] for i in range(2)]
    keys = [new("fl", 48) for t in range(ROUNDS)]
    xs = [x0] + [new("ul", 48) for t in range(ROUNDS)]
    toffs = [new("ul", 8) for t in range(ROUNDS + 1)]

    def ends(sc, a, b):
        return sub(sc, a + 15, b, 16)

    def group(out, row):
        scan(out, sub(mask, 0, out[2] - out[1]), row, A.add, A.min)

    def lists(t, sc, ssc):
        d = dx[t]
        n1, mx, n2, ky = new("fl", 48), new("fl", 48), new("fl", 48), new("fl", 48)
        tw = sub(d, 2, 144, 3)
        return [lambda: ts(tw, ends(sc, 0, 768), cp, A.add),
                lambda: ts(sub(d, 146, 240, 3), ends(sc, 0, 512), cp, A.add),
                lambda: ts(n1, tw, -8192.0, A.mult, 8192.0 * 1023, A.add),
                lambda: ts(toffs[t], ends(ssc, 0, 128), cp, A.add),
                lambda: tt(mx, n1, own, A.max),
                lambda: tt(fa[t], sub(d, 98, 240, 3), c1, A.add),
                lambda: tt(ky, mx, tw, A.add),
                lambda: tt(fb[t], sub(d, 50, 192, 3), tw, A.subtract),
                lambda: ts(n2, tw, -2.0 ** 24, A.mult, 2.0 ** 24 * 1023, A.add),
                lambda: tt(keys[t], ky, n2, A.min)]

    def pick_u(t):
        off = blk(uo, t, 8)
        c, d = 128 * t, 128 * t + 128
        run("v", lambda: g.vector.tensor_copy(T.qp[:, c:d].bitcast(dt.uint32), T.qu[:, 0:128].bitcast(dt.uint32).indirect(ap(off))),
            [("qp", c, d)], [("qu", 0, 128), uo])
        run("s", lambda: g.scalar.activation(T.sp[:, c:d], T.su[:, 0:128].indirect(ap(off)), AF.Copy), [("sp", c, d)], [("su", 0, 128), uo])

    sc0, scs = new("hl", 768), new("hl", 128)
    cut = OPT.get("cut", 40)

    def fills():
        fill(full("ec", 528), 0.0)
        fill(sub(pos, 256, 384), 512.0)
        fill(gz, 0.0)
        fill(dy, 1024.0)
        fill(keep, 1.0)

    def codes(q, k):
        if q == "s":
            scopy(sub(natinv, k, 768, 3), base, float(k), 4.0)
        else:
            ts(sub(natinv, k, 768, 3), base, 4.0, A.mult, float(k), A.add)

    def the_mask():
        ts(blk(mk, 0, 128), jrow, icol, A.is_lt, 8192.0, A.mult)
        ts(blk(mk, 1, 128), jrow, icol, A.is_equal, -2048.0, A.mult)
        for h in range(2):
            tt(blk(mask, h, 128), blk(mk, 0, 128), blk(mk, 1, 128), A.add)

    def after(row):
        for k in range(3):
            scopy(sub(ntn, (k + 2) % 3, 1024, 4), row[k])
    first = lists(0, sc0, scs)
    steps = {"fills": fills, "keep": lambda: ts(sub(keep, 0, 48, 3), sub(gz, 0, 16), 0.0, A.mult),
             "c0": lambda: codes("s", 0), "c1": lambda: codes("s", 1), "c2": lambda: codes("s", 2), "C2": lambda: codes("v", 2),
             "cs": lambda: scopy(sub(natinv, 768, 896), sub(base, 0, 128), 1025.0, 4.0),
             "and": lambda: ts(icol_i, pcol, 15, A.bitwise_and), "icol": lambda: vcopy(icol, icol_i),
             "cq": lambda: ts(cq, icol_i, 15.0, A.is_equal, -2048.0, A.mult), "ic4": lambda: ts(ic4, icol_i, 4.0, A.mult),
             "cols": lambda: ts(cols, sub(base, 3, 7), 512.0, A.mult, cq, A.add), "mask": the_mask,
             "uo": lambda: vcopy(uo, uo_i), "ids": lambda: ts(ids, id_i, ic4, A.add),
             "two": lambda: vcopy(tw_o, full("twi", 56)),
             "tr": lambda: sget(sub(trn, 0, 16 * cut), natinv, sub(tw_o, 0, cut)),
             "TR": lambda: vget(sub(trn, 16 * cut, 896), natinv, sub(tw_o, cut, 56)) if cut < 56 else None,
             "x0": lambda: ts(x0, full("twi", 48), -1.0, A.add, 1.0 / 3.0, A.mult),
             "own": lambda: ts(own, ids, -8192.0, A.mult, 8192.0 * 1023, A.add), "one": lambda: ts(c1, ids, -1.0, A.mult, 1024.0, A.add),
             "ec": lambda: ts(("ec", 3, 515, 4), sub(base, 0, 128), pf, A.is_equal),
             "qu": lambda: quant(full("qu", 128), full("su", 128), full("uin", 512)), "pick": lambda: pick_u(0),
             "qx": lambda: quant(full("qx", 256), full("sx", 256), full("xin", 1024)),
             "gs": lambda: group(scs, sub(trn, 768, 896)), "after": lambda: after([sub(trn, k, 768, 3) for k in range(3)]),
             "h0": lambda: scopy(sub(ntn, 3, 1024, 4), base), "h1": lambda: scopy(sub(f, 3, 1024, 4), base)}
    for k in range(4):
        steps["t%d" % k] = (lambda k: lambda: scopy(sub(tab, 1024 + k, 2048, 4), base, float((k + 2) % 3), 4.0))(k)
        steps["e%d" % k] = (lambda b: lambda: quant(reg("qe", b, 128), reg("se", b, 128), ("ec", 3 - b, 515 - b)))(k)
        steps["g%d" % k] = (lambda k: lambda: group(blk(sc0, k), sub(trn, k, 768, 3)))(k)
    for k in range(10):
        steps["l%d" % k] = first[k]
    start = steps

    def do(names):
        for name in names.split():
            start[name]()
    do(OPT.get("o1", "fills keep cs c0 C2 and c1 t0 uo cq t1 icol ic4 two x0 cols tr TR ids ec qu mask pick one qx g1 after"))
    dma("y", T.qw[:, :].bitcast(dt.uint8), T.wc[:, :], [full("qw", 512)], [], "ld3")
    dma("y", T.sw[:, :], T.ws[:, :], [full("sw", 512)], [], "ld4")

    def split(src):
        r = cores.index(src)
        a, b = topo.engines(src, cores[(r + 1) % n]), topo.engines(src, cores[(r + n - 1) % n])
        if len(a) <= len(b):
            return a, [e for e in b if e not in a]
        return [e for e in a if e not in b], b

    e_up, e_down = split(core)
    n_from = len(split(up)[1]) + len(split(down)[0])

    def transfer(c, es, sem, views):
        rid, pid, _s = topo.addr(c)
        return RemoteDMATransfer(dst_ids=[DstId(rid=rid, pnc=pid)], dma_engine_mask=sum(1 << e for e in es), remote_sem=T.sem[sem],
                                 srcs=[views[1]], dsts=[views[0]])

    def send(to_up, to_down, reads, sem):
        wait_for("g", needs("g", True, reads, []))
        total["loc"] = total.get("loc", 0) + len(e_up) + len(e_down)
        g.remote_dma_fused([transfer(up, e_up, sem, to_up), transfer(down, e_down, sem, to_down)], local_sem=T.sem.loc)
        note("g", True, reads, [], {"sem": "loc", "cnt": total["loc"], "clk": dict(known["g"])})

    def send_state(t):
        q, s = reg("qx", t, 256), reg("sx", t, 256)
        lo, hi = 2 * t, 2 * t + 1
        send((u8(reg("lq", hi, 256)), u8(q)), (u8(reg("lq", lo, 256)), u8(q)), [q], "aq%d" % t)
        send((ap(reg("lsc", hi, 256)), ap(s)), (ap(reg("lsc", lo, 256)), ap(s)), [s], "aq%d" % t)

    for t in range(ROUNDS):
        arrive("aq%d" % t, 2 * n_from, [reg("lq", t, 512), reg("lsc", t, 512)])
        arrive("al%d" % t, n_from, [reg("lnd", t, 8)])

    def score(t):
        mm(4, reg("qp", t, 128), reg("sp", t, 128), reg("qx", t, 256), reg("sx", t, 256), 256)

    def signs(q, out, scores):
        if q == "v":
            ts(out, scores, 0.0, A.is_gt, 1024.0, A.mult)
        else:
            run("s", lambda: g.scalar.activation(ap(out), ap(scores), AF.Sign, bias=-(2.0 ** -110)), [out], [scores])

    def zreg(t, b, a, e):
        return ("z", (4 * t + b) * ZW + a, (4 * t + b) * ZW + e)

    score(0)
    send_state(0)
    iota(sub(tab, 0, 1024), [[1, 1024]], 0, 0, True)
    iota(sub(f, 1024, 1536), [[1, 512]], 1024, 0, True)
    nsc = sc0
    do(OPT.get("o2", "g2 g0"))

    for t in range(ROUNDS):
        last = t == ROUNDS - 1
        po, spos, so = new("hl", 768), new("hl", 256), new("hl", 768)
        if t == 0:
            signs(OPT.get("p0", "v"), sub(pos, 0, 256), ("ps", 2048, 2304))
            part = [sub(po, k, 768, 3) for k in range(3)]
            sget(po, pos, xs[0])
            group(spos, sub(pos, 0, 256))
            do(OPT.get("o3", "l0 l1 gs e3 h1 t3 own h0 l2 l3 e1 e2 l4 e0 l8 l6 l7 l5 l9 t2"))
        else:
            part = [blk(po, k) for k in range(3)]
            group(spos, sub(pos, 0, 256))
            for k in range(3):
                get["ssv"[k]](part[k], pos, blk(xs[t], k, 16))
        for b in range(4):
            mm(b, reg("qe", b, 128), reg("se", b, 128), reg("qx", t, 256), reg("sx", t, 256), 256)
        for b in range(4):
            scopy(zreg(t, b, 0, 256), ("ps", 512 * b, 512 * b + 256))
        wants, pk, rk = new("fl", 48), new("fl", 48), new("fl", 48)
        sign = {"s": lambda k: group(blk(so, k), part[k]),
                "w": lambda k: tt(blk(wants, k, 16), ends(so, 256 * k, 256 * k + 256), ends(spos, 0, 256), A.not_equal),
                "p": lambda k: tt(sub(pk, k, 48, 3), blk(wants, k, 16), blk(keys[t], k, 16), A.mult)}
        for step in (OPT.get("sorder", "s0 s2 w0 w2 s1 p0 w1 p2 p1") if t else "s0 s1 s2 w0 w1 w2 p0 p1 p2").split():
            sign[step[0]](int(step[1]))
        scan(rk, keep, pk, A.mult, A.max)
        r = sub(rk, 2, 48, 3)
        m_o, r_i, c_i, oc, cn, rd = new("ul", 16), new("il", 16), new("il", 16), new("ul", 16), new("ul", 16), new("fl", 16)
        ts(m_o, r, 1.0 / 8192, A.mult)
        vcopy(r_i, r)
        rr = new("fl", 256)
        ro, rs, tq, tqs = [new("hl", 256) for i in range(4)]
        fz = OPT.get("fz", 0)
        sget(rr, sub(tab, 0, 1024), m_o)
        icx = [sub(gz, 48 * i + 1, 48 * i + 48, 3) for i in range(4)]
        tt(icx[0], blk(keys[t], 1, 16), r, A.is_equal)
        tt(icx[1], blk(keys[t], 2, 16), r, A.is_equal)
        ts(c_i, r_i, 2047, A.bitwise_and)
        tt(icx[2], blk(keys[t], 0, 16), r, A.is_equal)
        tt(icx[3], blk(keys[t], 1, 16), r, A.is_equal)
        ts(oc, c_i, QUARTER, A.mult)
        vcopy(cn, c_i)
        if not fz:
            sget(ro, rr, oc)
        tqv = OPT.get("tqv", 0)
        if not tqv:
            sget(tq, ntn, cn)
        ia = sub(gz, 49, 192, 3)
        if fz == 1:
            run("v", lambda: g.vector.tensor_tensor(ap(ro), ap(rr).indirect(ap(oc)), ap(rr), A.is_equal), [ro], [rr, oc])
        if not fz:
            ts(rd, m_o, cp, A.subtract)
        tt(sub(dy, 1, 144, 3), fa[t], ia, A.mult)
        tt(sub(dx[t], 1, 144, 3), fb[t], ia, A.mult)
        if fz == 2:
            run("v", lambda: g.vector.tensor_tensor(ap(ro), ap(rr).indirect(ap(oc)), ap(rr), A.is_equal), [ro], [rr, oc])
        if tqv:
            vget(tq, ntn, cn)
        for b in range(4):
            mm(4 + b, reg("qe", b, 128), reg("se", b, 128), reg("lq", t, 512), reg("lsc", t, 512), 512)
        ys, yo, xx, xo = new("hl", 144), new("ul", 48), new("hl", 144), new("ul", 48)
        nts, ssc, sd = new("hl", 128), new("hl", 128), new("snd", 8)
        old, nth, nsc = nsc, new("hl", 768), new("hl", 768)
        x = xs[t + 1]
        nf = OPT.get("nf", 32)
        nn = OPT.get("nn", 28)

        def expand(q, a, b):
            while a < b:
                k, e = a // 16, min(b, a // 16 * 16 + 16)
                get[q](sub(f, k + 64 * (a - 16 * k), 64 * (e - 16 * k), 4), tab, sub(yo, a, e))
                a = e

        def flags():
            for k in range(3):
                if fz:
                    ts(sub(gz, 48 * k + 2, 48 * k + 48, 3), ends(rs, 0, 256), cp, A.add)
                else:
                    tt(sub(gz, 48 * k + 2, 48 * k + 48, 3), ends(rs, 0, 256), rd, A.is_equal)

        def changes():
            for k in range(3):
                tt(sub(dx[t], 48 * k, 48 * k + 48, 3), ends(tqs, 0, 256), ends(old, 256 * k, 256 * k + 256), A.subtract)

        def post():
            ts(sub(sd, 0, 4), ends(ssc, 0, 64), cpm, A.add, QUARTER, A.mult)
            ts(sub(sd, 4, 8), ends(ssc, 64, 128), cp, A.add, QUARTER, A.mult)
            send((ap(reg("lnd", 2 * t + 1, 4)), ap(sub(sd, 0, 4))), (ap(reg("lnd", 2 * t, 4)), ap(sub(sd, 4, 8))), [sd], "al%d" % t)
        steps = {"rs": lambda: group(rs, ro), "go": flags,
                 "ys": lambda: scan(ys, sub(gz, 0, 144), dy, A.mult, A.add), "yo": lambda: vcopy(yo, sub(ys, 2, 144, 3)),
                 "f": lambda: expand("s", 0, nf), "F": lambda: expand("v", nf, 48),
                 "tq": lambda: group(tqs, tq), "ux": changes,
                 "xx": lambda: scan(xx, sub(gz, 0, 144), sub(dx[t], 0, 144), A.mult, A.add), "xo": lambda: vcopy(xo, sub(xx, 2, 144, 3)),
                 "SL": lambda: vget(nts, f, toffs[t]), "sl": lambda: sget(nts, f, toffs[t]),
                 "ss": lambda: group(ssc, nts), "post": post,
                 "n": lambda: sget(sub(nth, 0, 16 * nn), f, sub(xo, 0, nn)), "N": lambda: vget(sub(nth, 16 * nn, 768), f, sub(xo, nn, 48)),
                 "x": lambda: ts(x, ends(nsc, 0, 768), cp, A.add, QUARTER, A.mult)}
        for k in range(3):
            steps["n%d" % k] = (lambda k: lambda: sget(blk(nth, k), f, blk(xo, k, 16)))(k)
            steps["N%d" % k] = (lambda k: lambda: vget(blk(nth, k), f, blk(xo, k, 16)))(k)
            steps["s%d" % k] = (lambda k: lambda: group(blk(nsc, k), blk(nth, k)))(k)
        nothing = lambda: None
        if last:
            cl, s_o, otb = new("ul", 48), new("ul", 8), new("fl", 896)
            later = [lambda: ts(cl, ends(nsc, 0, 768), cp, A.add), lambda: quant(full("qv", 128), full("svp", 128), full("vin", 512)),
                     nothing, lambda: ts(s_o, ends(ssc, 0, 128), cp, A.add),
                     lambda: vget(sub(otb, 0, 768, 3), nattab, blk(cl, 0, 16)), nothing,
                     nothing, nothing, nothing, lambda: vget(sub(otb, 1, 768, 3), nattab, blk(cl, 1, 16))]
        else:
            later = lists(t + 1, nsc, ssc)
        tb = 1024 * t
        win = [zreg(t, b, 0, ZW) for b in range(4)]
        outs = [("mt", tb + b, tb + 1024, 4) for b in range(4)]
        ma, mb = [reg("ma", 4 * t + b, 256) for b in range(4)], [reg("mb", 4 * t + b, 256) for b in range(4)]
        mg, ms = [reg("mg", 2 * t + b % 2, 768) for b in range(4)], [reg("ms", 2 * t + b % 2, 768) for b in range(4)]

        def once():
            if t == 0:
                dma("y", T.vin[:, :], T.v[:, :], [full("vin", 512)], [x], "ld5")
                for k in range(3):
                    ts(("m3", k, 768, 3), mask, 0.0, A.mult, 0.0 if k else -1.0e29, A.add)

        def numbers():
            if last:
                sget(sub(otb, 2, 768, 3), nattab, blk(cl, 2, 16))
                sget(sub(otb, 768, 896), nattab, s_o)

        def half(h):
            c0 = tb + 4 * HW * h
            w = HW // 16
            steps["O1" + "ab"[h]] = lambda: vmax(("mt", c0 + 1, c0 + 4 * HW, 4), win[1], sub(x, 32 + w * h, 32 + w * h + w), blk(mb[1], h, HW))
            steps["C3" + "ab"[h]] = lambda: vcopy(("mt", c0 + 3, c0 + 4 * HW, 4), sub(ms[3], 3 * HW * h + 2, 3 * HW * (h + 1), 3))
            steps["p" + "ab"[h]] = lambda: quant(reg("qm", H * t + h, HW), reg("sm", H * t + h, HW), reg("mt", H * t + h, 4 * HW))
        for h in range(H):
            half(h)
        by_b = {"U": lambda b: vcopy(reg("nz", 4 * t + b, 512), reg("ps", 4 + b, 512)),
                "u": lambda b: scopy(reg("nz", 4 * t + b, 512), reg("ps", 4 + b, 512)),
                "B": lambda b: vget(zreg(t, b, 256, 384), reg("nz", 4 * t + b, 512), reg("lnd", t, 8)),
                "b": lambda b: sget(zreg(t, b, 256, 384), reg("nz", 4 * t + b, 512), reg("lnd", t, 8)),
                "G": lambda b: vget(ma[b], win[b], blk(x, 0, 16)),
                "g": lambda b: sget(ma[b], win[b], blk(x, 0, 16)),
                "M": lambda b: vmax(mb[b], win[b], blk(x, 1, 16), ma[b]),
                "O": lambda b: vmax(outs[b], win[b], blk(x, 2, 16), mb[b]),
                "i": lambda b: sget(sub(mg[b], 0, 768, 3), win[b], blk(x, 0, 16)),
                "j": lambda b: sget(sub(mg[b], 1, 768, 3), win[b], blk(x, 1, 16)),
                "k": lambda b: sget(sub(mg[b], 2, 768, 3), win[b], blk(x, 2, 16)),
                "R": lambda b: scan(ms[b], full("m3", 768), mg[b]),
                "C": lambda b: vcopy(outs[b], sub(ms[b], 2, 768, 3))}
        for name in by_b:
            for b in range(4):
                steps[name + str(b)] = (lambda fn, b: lambda: fn(b))(by_b[name], b)
        for k in range(10):
            steps["l%d" % k] = later[k]
        steps.update({"once": once, "ot": numbers, "pick": nothing if last else lambda: pick_u(t + 1)})
        def layer(h):
            for b in range(4):
                mm(4 + b, reg("qw", b, 128), reg("sw", b, 128), reg("qm", H * t + h, HW), reg("sm", H * t + h, HW), HW)
            for b in range(4):
                tmp, wb = reg("tm", H * b + h, HW), ("ps", 2048 + 512 * b, 2048 + 512 * b + HW)
                run("s", lambda: g.scalar.activation(ap(tmp), ap(wb), AF.Relu, scale=0.015625), [tmp], [wb])

        def state(h):
            c0 = tb + 4 * HW * h
            for b in range(4):
                tt(("xt", c0 + b, c0 + 4 * HW, 4), reg("tm", H * b + h, HW), ("ps", 512 * b + HW * h, 512 * b + HW * h + HW), A.add)

        def pack(h):
            q = reg("qx", H * (t + 1) + h, HW)
            quant(q, reg("sx", H * (t + 1) + h, HW), reg("xt", H * t + h, 4 * HW))
            if last:
                dma("y", T.oc[:, 4 * HW * h:4 * HW * (h + 1)], u8(q), [], [q], "out")
            if h == H - 1 and not last:
                send_state(t + 1)

        def scores(h, q):
            w, ws = (full("qv", 128), full("svp", 128)) if last else (reg("qp", t + 1, 128), reg("sp", t + 1, 128))
            mm(4 + h, w, ws, reg("qx", H * (t + 1) + h, HW), reg("sx", H * (t + 1) + h, HW), HW)
            got = ("ps", 2048 + 512 * h, 2048 + 512 * h + HW)
            if last:
                copy["sv"[h]](reg("yo", h, HW), got)
                dma("sy"[h], T.y[:, HW * h:HW * h + HW], ap(reg("yo", h, HW)), [], [reg("yo", h, HW)], "out")
            else:
                signs(q, blk(pos, h, HW), got)

        def tables():
            if t == 0:
                iota(sub(nattab, 0, 1024), [[3, 256], [1, 4]], 0, 0, True)
            if t == 1:
                iota(sub(nattab, 1024, 1536), [[1, 128], [0, 4]], 768, 0, True)
            if last:
                dma("y", T.ot[:, :], T.fl[0:128:16, otb[1]:otb[2]], [], [otb], "out")
        for h in range(H):
            for name, fn in (("r", layer), ("A", state), ("Q", pack), ("z", lambda h: scores(h, "s")), ("Z", lambda h: scores(h, "v"))):
                steps[name + "ab"[h]] = (lambda fn, h: lambda: fn(h))(fn, h)
        for k in range(3):
            steps["a%d" % k] = nothing if last else (lambda k: lambda: scopy(sub(ntn, (k + 2) % 3, 1024, 4), blk(nth, k)))(k)
        steps["tab"] = tables
        for step in OPT.get("forder", "rs go ys tq yo f ux F xx xo SL n ss post N s0 s2 s1 x u0 u1 u2 u3 l0 once l2 l3 l1 l4 l8 l6 l5 l7 l9 b2 g2 b3 B0 B1 G0 M2 g1 i3 j3 k3 M0 O2 M1 O0 R3 ot O1a C3a C3b pa O1b pick pb tab ra Aa rb a0 a1 a2 Qa Ab Qb Za Zb").split():
            steps[step]()

    q, s = reg("qx", ROUNDS, 256), reg("sx", ROUNDS, 256)
    for k in range(4):
        dma("y" if k % 2 else "s", T.osc[4 * k:4 * k + 4, :], T.sx[32 * k:32 * k + 4, s[1]:s[2]], [], [s], "out")
    for s in sorted(total):
        if known["g"].get(s, 0) < total[s]:
            g.wait_ge(T.sem[s], total[s])
